import numpy as np, ml_dtypes
CORES = [66,74,82,90,194,202,210,218]
N = 8
BF = ml_dtypes.bfloat16
W, L, B, CAP, C, S, RO = 2048, 256, 8, 64, 8, 32, 4
def work(rng, *shape):
    return B * rng.integers(0, L, shape) + rng.integers(0, RO, shape)
def land(rng, *shape):
    return S * rng.integers(0, CAP, shape) + RO + rng.integers(0, RO, shape)
def parts(rng):
    X = rng.integers(0, 256, (N, 8, 16, W)); R = rng.integers(0, W, (N, 8, 16, W)); R = np.where(rng.random(R.shape) < 0.5, R[:, :, :1], R)
    z = rng.random((N, 8, W)); A = np.where(z < 0.3, work(rng, N, 8, W), np.where(z < 0.5, land(rng, N, 8, W), rng.integers(0, W, (N, 8, W))))
    return X, R, A, rng.integers(0, 256, (N, 8, 16)), rng.integers(1000, 1250, (N, 8, 1)) + rng.integers(0, 200, (N, 8, 16))
def pack(X, R, A, w, th):
    return {"xc": np.ascontiguousarray(X.reshape(N, 128, W)).astype(np.float32).astype(BF), "rf": np.ascontiguousarray(R.reshape(N, 128, W)).astype(np.int32),
            "an": np.ascontiguousarray(A).astype(np.int32), "w": w.reshape(N, 128, 1).astype(np.int32), "th": th.reshape(N, 128, 1).astype(np.int32)}
def setup_inputs(rng):
    return pack(*parts(rng))
def setup_inputs_copies(rng):
    X, R, A, w, th = parts(rng); x = np.arange(W)
    R[:, 1::4] = np.repeat(R[:, 1::4, :1], 16, axis=2)
    R[:, 2::4, 1:] = (R[:, 2::4, :1] + rng.integers(1, W, (N, 2, 15, W))) & (W - 1)
    A[:, ::2] = (x - B) & (W - 1)
    A[:, 1::2] = np.where(rng.random((N, 4, W)) < 0.5, land(rng, N, 4, W), work(rng, N, 4, W))
    th = rng.choice(np.array([1100, 1300, 1500]), (N, 8, 1)) + rng.integers(0, 200, (N, 8, 16))
    return pack(X, R, A, w, th)
def setup_inputs_corners(rng):
    X, R, A, w, th = parts(rng); kk = np.arange(16).reshape(1, 1, 16, 1); x = np.arange(W); heads = B * np.arange(L); off = x & (B - 1)
    X = rng.integers(0, 4, (N, 8, 16, W)); R = rng.integers(0, W, (N, 8, 16, W))
    first = R[:, :, :1]; first = np.where((first & (B - 1)) == 0, first ^ 1, first)
    R = np.where((rng.random(R.shape) < 0.5) | (kk == 0), first, R)
    R = np.where(((R + 613 * kk) & (B - 1)) == 0, R ^ 1, R)
    th = rng.integers(49, 101, (N, 8, 16)); slow = []
    for q in range(N):
        for g in range(8):
            k = int(rng.choice(np.array([0, 1, CAP - 1, CAP, CAP + 1, L])))
            if q == 0: k = (CAP, CAP + 1, L, CAP - 1, 1, 0, CAP, CAP + 1)[g]
            if q == 1: k = (CAP, CAP - 1, 1, 0, 0, 0, 0, 256 - 2 * CAP)[g]
            if q == 2: k = 31 + int(g < 7)
            if q == N - 1 and g == 7: k = CAP
            o = rng.permutation(L)
            if g == 7 and k > 0:
                i = int(np.flatnonzero(o < k)[-1]); o[[i, L - 1]] = o[[L - 1, i]]
            go = o < k; h = np.where(go, 0, rng.integers(100, 256, (16, L))); near = rng.integers(10, 13, (16, L))
            if q == 1: h = np.where(~go & (rng.random(L) < 0.5), near, h)
            if q == 2:
                h = np.where(o < 56, 0, np.where(o < 186, near, h)); slow.append(heads[(o >= k) & (o < 186)])
            X[q, g][:, heads] = h
    w[:, 0::4] = 255; w[:, 1::4] = 0; w[1:3] = 0
    A[:, 0] = x; A[:, 1] = (W - 1) * rng.integers(0, 2, (N, W)); A[:, 2] = (x + 1) & (W - 1); A[:, 3] = (x - B) & (W - 1); A[:, 5] = (x - 1) & (W - 1)
    A[:, 6] = np.where(rng.random((N, W)) < 0.5, x, W - 1 - x)
    X[2][:, :, off == 1] = rng.integers(100, 256, (8, 16, L))
    to = B * rng.integers(0, L, (8, 16, W)) + np.where(off == 2, 1, rng.integers(2, B, (8, 16, W)))
    R[2] = (to - 613 * kk[0]) & (W - 1)
    A[2] = B * rng.integers(0, L, (8, W)) + 3
    A[2][:, 2 * B * np.arange(L // 2) + 2] = 2 * B * rng.integers(0, L // 2, (8, L // 2)) + B + 2
    for g in range(8): A[2, g, slow[g]] = 2 * B * rng.integers(0, L // 2, len(slow[g])) + 2
    return pack(X, R, A, w, th)
def setup_inputs_ends(rng):
    kind = rng.integers(0, 3, (N, 8, 1, W)); X = 255 * np.where(kind == 2, rng.integers(0, 2, (N, 8, 16, W)), kind)
    R = (W - 1) * rng.integers(0, 2, (N, 8, 16, W)); A = (W - 1) * rng.integers(0, 2, (N, 8, W))
    z = rng.random((N, 8, W)); A = np.where(z < 0.12, work(rng, N, 8, W), np.where(z < 0.25, land(rng, N, 8, W), A))
    w = 255 * rng.integers(0, 2, (N, 8, 16)); th = np.zeros((N, 8, 16), np.int64)
    for q in range(N):
        many = np.append(rng.permutation(np.array([C, C - 1, C - 2, C + 1, C - 1, C, C - 1])), C)
        i = int(np.flatnonzero(many == C)[0]); many[[i, 6]] = many[[6, i]]
        for g in range(8): th[q, g, rng.permutation(16)[:many[g]]] = 4080
    w[:, 7] = 255; w[:, 6] = 0; w[:, 6, 0] = 255; w[:, 6, 1] = 1
    for x in (0, W - B):
        X[:, 7, :, x] = 255; A[:, 7, x] = 0
    X[:, 6, 0, W - B] = 16; X[:, 6, 1, W - B] = 15; A[:, 6, W - B] = W - 1; R[:, 6, 0, W - B] = 0
    X[:, 6, 0, 0] = 15; X[:, 6, 1, 0] = 250; A[:, 6, 0] = W - 2; R[:, 6, 0, 0] = 0
    R[:, 6, :, W - 1] = W - 1
    R[:, 6, :, W - 2] = W - 3
    R[:, 7, 0, 0] = W - 1; R[:, 7, 14:, 0] = 0
    X[:, 7, :, (613 * 15) & (W - 1)] = 0; X[:, 7, :, (613 * 14) & (W - 1)] = 255
    return pack(X, R, A, w, th)
def setup_inputs_spread(rng):
    X = (rng.random((N, 8, 16, W)) * np.exp2(rng.integers(0, 9, (N, 8, 1, W)))).astype(np.int64)
    p = rng.choice(np.array([1, 2, 4]), (N, 8, 16, 1)); R = np.minimum((W * rng.random((N, 8, 16, W)) ** p).astype(np.int64), W - 1)
    R = np.where(rng.random(R.shape) < rng.random((N, 8, 1, W)), R[:, :, :1], R)
    p = rng.choice(np.array([1, 2, 4]), (N, 8, 1)); A = np.minimum((W * rng.random((N, 8, W)) ** p).astype(np.int64), W - 1)
    w = np.minimum(np.exp2(8 * rng.random((N, 8, 16))).astype(np.int64), 255) * (rng.random((N, 8, 16)) > 0.1)
    p = rng.choice(np.array([1, 2, 4, 8]), (N, 8, 1)); th = np.minimum((4081 * rng.random((N, 8, 16)) ** p).astype(np.int64), 4080)
    return pack(X, R, A, w, th)
def setup_inputs_ties(rng):
    X, R, A, w, th = parts(rng)
    pool = rng.integers(0, 256, (N, 8, 16, 6)); X = np.take_along_axis(pool, rng.integers(0, 6, (N, 8, 1, W)), 3)
    i = rng.integers(0, 6, (N, 8, 1, 16)); j = rng.integers(0, 6, (N, 8, 1, 16))
    d = np.add.reduce(np.abs(np.take_along_axis(pool, i, 3) - np.take_along_axis(pool, j, 3)), axis=2)
    return pack(X, R, A, w, np.minimum(d + rng.integers(0, 2, d.shape), 4080))
def check_inputs(d):
    bad = []
    for k, lo, hi in (("xc", 0, 255), ("rf", 0, W - 1), ("an", 0, W - 1), ("w", 0, 255), ("th", 0, 4080)):
        a = np.asarray(d[k]).astype(np.float64)
        if not (np.min(a) >= lo and np.max(a) <= hi): bad.append("range of " + k)
        elif np.any(a != np.floor(a)): bad.append("whole numbers in " + k)
    return bad
def cols(T, ix):
    return np.take_along_axis(T, ix[:, :, None, :], 3)
def dist(X, q, u, m):
    kk = np.arange(16).reshape(1, 1, 16, 1); s = ((m * u >> 5) + m + 613 * kk) & (W - 1)
    x = cols(X, s.reshape(N, 8, 16 * L)).reshape(N, 8, 16, 16, L)
    return np.add.reduce(np.abs(x - q[:, :, :, None, :]), axis=2).astype(np.int64)
def reference(xc, rf, an, w, th):
    X = xc.astype(np.float32).astype(np.int32).reshape(N, 8, 16, W); R = rf.astype(np.int64).reshape(N, 8, 16, W); A = an.astype(np.int64)
    ww = w.astype(np.int64).reshape(N, 8, 16, 1); tt = th.astype(np.int64).reshape(N, 8, 16, 1)
    v = np.zeros((N, 8, 1), np.int64) + B * np.arange(L); a = np.take_along_axis(A, v, 2); b = np.zeros((N, 1, 1, 1), np.int64)
    for t in range(RO):
        q = cols(X, v); u = np.add.reduce(ww * q, axis=2, keepdims=True) & 4095
        e = cols(R, a); own = np.take_along_axis(R[:, :, 0], v, 2)[:, :, None, :]
        n = np.where(e == e[:, :, :1], own, e)
        d, d2 = dist(X, q, u, e), dist(X, q, u, n)
        f = np.where(d2 < d, n, e); f[:, :, 0] = own[:, :, 0]
        fit = (np.add.reduce((np.minimum(d, d2) < tt + b).astype(np.int64), axis=2) >= C).astype(np.int64)
        b = (np.add.reduce(fit, axis=(1, 2)) & 255).reshape(N, 1, 1, 1)
        after = np.where(fit == 1, np.take_along_axis(A, v + 1, 2), np.take_along_axis(A, a, 2))
        r, g, i = np.nonzero(fit)
        R[r, g, :, v[r, g, i]] = f[r, g, :, i]; A[r, g, v[r, g, i]] = a[r, g, i]
        before = np.add.accumulate(fit, axis=2) - fit
        r, g, i = np.nonzero((fit == 1) & (before < CAP))
        R[(r + 1 + t % (N - 1)) % N, g, :, S * before[r, g, i] + RO + t] = f[r, g, :, i]
        v = v + fit; a = after
    o = R.reshape(N, 8, 16, L, B); o = o[..., :RO // 2] + 4096 * o[..., RO // 2:RO]
    h = R.reshape(N, 8, 16, CAP, S)[..., RO:2 * RO]
    return {"yr": o.reshape(N, 128, L * (RO // 2)).astype(np.float32), "yh": h.reshape(N, 128, CAP * RO).astype(np.float32),
            "yan": A.reshape(N, 8, L, B)[..., :RO].reshape(N, 8, L * RO).astype(np.float32), "yv": v.astype(np.float32), "ya": a.astype(np.float32)}

@@ -1,0 +1,557 @@
+from concourse.mybir import AluOpType as OP, ActivationFunctionType as AF, AxisListType
+
+TW = 2048
+DUMP = 3072
+KV = 12
+KA = 4
+N1 = (0, 4, 4, 0)
+W1 = 1
+W0 = 0
+NG = 10
+PLAN = (("Vq", 0, 64), ("Vq", 64, 128), ("Vg", 128, 160), ("Sg", 192, 256), ("Q", 0, 64), ("Sg", 160, 192),
+        ("D", 192, 0), ("D", 224, 1), ("A", 192, 0), ("A", 224, 1), ("M", 0, 64), ("D", 128, 0), ("K",), ("D", 160, 1),
+        ("Q", 64, 128), ("M", 192, 256), ("A", 128, 0), ("A", 160, 1), ("M", 64, 128), ("M", 128, 192))
+SCRATCH = {}
+for _n, _w, _d in (
+    ("X2", 4096, "bfloat16"), ("R", 5120, "int32"), ("AA", 5120, "float32"), ("OWB", 2048, "float32"),
+    ("OWN", 1024, "float32"), ("U", 1024, "float32"), ("KN", 1024, "float32"), ("QS", 1024, "bfloat16"),
+    ("IOT", 2048, "float32"), ("SXF", 4096, "float32"), ("SXS", 2048, "float32"), ("MX", 4096, "bfloat16"),
+    ("QX", 2048, "bfloat16"), ("XG", 4096, "bfloat16"), ("DD", 4096, "bfloat16"), ("AD", 4096, "bfloat16"),
+    ("E", 2048, "bfloat16"), ("q", 256, "bfloat16"), ("u", 256, "float32"), ("kn", 256, "float32"),
+    ("ow", 256, "float32"), ("aB", 256, "float32"), ("AB", 512, "float32"), ("e", 256, "float32"),
+    ("prod", 256, "int32"), ("pl", 256, "int32"), ("pl16", 256, "uint16"), ("eqs", 256, "float32"),
+    ("xk", 256, "float32"), ("m", 256, "int32"), ("hit", 256, "bfloat16"), ("F", 264, "int32"),
+    ("fitb", 256, "float32"), ("cum", 256, "float32"), ("junk", 1024, "float32"), ("acc", 4, "float32"),
+    ("inv16", 8, "uint16"), ("QT", 256, "bfloat16"), ("wsx", 256, "float32"),
+    ("fit", 16, "float32"), ("nf", 16, "float32"), ("f256", 16, "float32"), ("Aw", 32, "float32"), ("dA", 16, "float32"),
+    ("tA", 16, "float32"), ("aw", 16, "float32"), ("vtw", 16, "float32"), ("vw", 16, "float32"), ("vsw", 16, "float32"),
+    ("AL", 32, "uint16"), ("VT16", 16, "uint16"), ("VS16", 16, "uint16"),
+    ("bsum", 1, "float32"), ("bI", 2, "int32"), ("th4", 1, "float32"), ("thb", 1, "float32"),
+    ("thI", 1, "int32"), ("wI", 1, "int32"), ("wF", 1, "float32"),
+    ("pI", 1, "int32"), ("pF", 1, "float32"), ("qI", 1, "int32"), ("q16", 1, "float32"), ("c15", 1, "float32"),
+    ("rI", 1, "int32"), ("rF", 1, "float32"), ("hI", 1, "int32"), ("m1", 1, "float32"), ("m0", 1, "float32"),
+    ("kI", 2, "int32"), ("ck", 1, "float32"),
+    ("jc", 4, "float32"), ("CI", 144, "float32"), ("CB", 128, "float32"), ("C16", 16, "float32"),
+    ("Z1", 144, "bfloat16"), ("Z4", 144, "bfloat16"), ("Z8", 144, "bfloat16"), ("ZW", 144, "bfloat16"), ("Z0F", 144, "float32"),
+    ("BO", 128, "bfloat16"), ("BOW", 128, "bfloat16"), ("BON", 128, "bfloat16"), ("B0", 128, "float32"),
+    ("ID", 128, "bfloat16"), ("NI", 128, "bfloat16"), ("IZ", 128, "float32"), ("I0", 128, "float32"),
+    ("IDF", 128, "float32"), ("ONF", 144, "float32"),
+    ("ON", 256, "bfloat16"), ("CSE", 128, "bfloat16"), ("CSO", 128, "bfloat16"),
+    ("AC", 128, "int32"), ("OC", 128, "int32"), ("ACF", 128, "float32"), ("OCF", 128, "float32"),
+    ("TI", 160, "float32"), ("TT", 160, "float32"), ("t0", 80, "float32"), ("t1", 80, "float32"), ("WW", 80, "float32"),
+    ("uI", 256, "int32"), ("uA", 256, "int32"), ("uwI", 64, "int32"), ("uwA", 64, "int32"), ("uwF", 64, "float32"),
+    ("pr", 64, "int32"), ("bs", 64, "int32"), ("OL", 1024, "uint16"), ("bt", 64, "int32"),
+    ("YR", 512, "float32"), ("YH", 256, "float32"), ("YA", 1024, "float32"),
+    ("YV", 256, "float32"), ("YL", 256, "float32"),
+    ("SND", 256, "int32"), ("ARR", 256, "int32"),
+):
+    SCRATCH[_n] = ("sbuf", [128, _w], _d)
+PS = ("pK", "pE", "pO", "pD0", "pD1", "pC", "pW")
+for _n in PS:
+    SCRATCH[_n] = ("psum", [128, 512], "float32")
+SCRATCH["pT"] = ("psum", [128, 1024], "bfloat16")
+PSUM = PS + ("pT",)
+DMAS = {"lAC": 1, "lOC": 1, "lWT": 2, "lX": 1, "lXb": 1, "lR": 1, "gOW": 16, "gAA": 16, "gSF": 1, "gSX": 16,
+        "oR": 1, "oH": 1, "oA": 1, "oV": 1, "oL": 1}
+SEMAPHORES = ["V", "S", "P", "G", "snd"] + ["arr%d" % t for t in range(4)] + list(DMAS)
+
+
+def _meet(a, b):
+    if a[0] >= b[1] or b[0] >= a[1]:
+        return False
+    if a[2] == b[2]:
+        return a[2] == 1 or (a[0] - b[0]) % a[2] == 0
+    if a[2] == 1 or b[2] == 1:
+        if b[2] == 1:
+            a, b = b, a
+        first = b[0] + max(0, -((b[0] - a[0]) // b[2])) * b[2]
+        return first < min(a[1], b[1])
+    return True
+
+
+def _covers(a, b):
+    return a == b or (a[2] == 1 and a[0] <= b[0] and a[1] >= b[1])
+
+
+def rank_program(g, core, T, topo):
+    rank = T.rank_of(core)
+    if rank is None:
+        return
+    N = len(T.cores)
+    Q = {"V": g.vector, "S": g.scalar, "P": g.tensor, "G": g, "Y": g.sync}
+    count = {k: 0 for k in "VSPG"}
+    known = {k: {} for k in Q}
+    log = {}
+
+    def r(name, lo=0, hi=None, st=1):
+        return (name, lo, SCRATCH[name][1][1] if hi is None else hi, st)
+
+    def ap(x):
+        if len(x) == 2:
+            return ap(x[0]).indirect(ap(x[1]))
+        n, lo, hi, st = x
+        return T[n][:, lo:hi:st] if st > 1 else T[n][:, lo:hi]
+
+    def flat(xs):
+        out = []
+        for x in xs:
+            if isinstance(x, tuple):
+                if len(x) == 2:
+                    out += [x[0], x[1]]
+                else:
+                    out.append(x)
+        return out
+
+    def learn(eng, sem, val, clock):
+        kn = known[eng]
+        if kn.get(sem, 0) >= val:
+            return
+        Q[eng].wait_ge(T.sem[sem], val)
+        for s, x in clock.items():
+            if kn.get(s, 0) < x:
+                kn[s] = x
+        kn[sem] = max(kn.get(sem, 0), val)
+
+    def op(eng, fn, reads, writes, grp=None):
+        reads, writes = flat(reads), flat(writes)
+        need = {}
+        for acc, wr in [(x, False) for x in reads] + [(x, True) for x in writes]:
+            bank = acc[0] in PSUM
+            for (sp, w2, eng2, sem, val, clock, grp2) in log.get(acc[0], ()):
+                if grp is not None and grp2 == grp:
+                    continue
+                if eng2 == eng and grp2 is None and grp is None:
+                    if (bank and eng == "P") or not (wr or w2) or not _meet(acc[1:], sp):
+                        continue
+                elif bank:
+                    pass
+                else:
+                    if not (wr or w2) or not _meet(acc[1:], sp):
+                        continue
+                if sem not in need or need[sem][0] < val:
+                    need[sem] = (val, clock)
+        for sem in sorted(need, key=lambda s: -len(need[s][1])):
+            learn(eng, sem, need[sem][0], need[sem][1])
+        ins = fn()
+        if grp is None:
+            count[eng] += 1
+            sem, val = eng, count[eng]
+            ins.then_inc(T.sem[sem], 1)
+        else:
+            sem, val = grp, 16 * DMAS[grp]
+            ins.then_inc(T.sem[sem], 16)
+        clock = dict(known[eng])
+        clock[sem] = val
+        for acc, wr in [(x, False) for x in reads] + [(x, True) for x in writes]:
+            old = log.setdefault(acc[0], [])
+            keep = []
+            for rec in old:
+                gone = False
+                if grp is None or rec[6] != grp:
+                    if wr and _covers(acc[1:], rec[0]):
+                        gone = True
+                    elif not wr and not rec[1] and rec[2] == eng and rec[6] is None and grp is None and _covers(acc[1:], rec[0]):
+                        gone = True
+                if not gone:
+                    keep.append(rec)
+            keep.append((acc[1:], wr, eng, sem, val, clock, grp))
+            log[acc[0]] = keep
+
+    def sc(x):
+        return ap(x) if isinstance(x, tuple) else x
+
+    def tt(o, a, b, f):
+        op("V", lambda: g.vector.tensor_tensor(out=ap(o), in0=ap(a), in1=ap(b), op=f), [a, b], [o])
+
+    def ts(o, a, s1, f, s2=None, f2=None):
+        if f2 is None:
+            op("V", lambda: g.vector.tensor_scalar(out=ap(o), in0=ap(a), scalar1=sc(s1), scalar2=None, op0=f), [a, s1], [o])
+        else:
+            op("V", lambda: g.vector.tensor_scalar(out=ap(o), in0=ap(a), scalar1=sc(s1), scalar2=sc(s2), op0=f, op1=f2), [a, s1, s2], [o])
+
+    def cp(o, a):
+        op("V", lambda: g.vector.tensor_copy(out=ap(o), in_=ap(a)), [a], [o])
+
+    def scatter(win, off, a):
+        op("V", lambda: g.vector.tensor_copy(out=ap((win, off)), in_=ap(a)), [a, off], [win])
+
+    def act(o, a, f=AF.Copy, bias=None, scale=None, acc=None):
+        kw = {}
+        if bias is not None:
+            kw["bias"] = sc(bias)
+        if scale is not None:
+            kw["scale"] = sc(scale)
+        if acc is not None:
+            kw["accum_out"] = ap(acc)
+        op("S", lambda: g.scalar.activation(out=ap(o), in_=ap(a), func=f, **kw), [a, bias, scale], [o] + ([acc] if acc else []))
+
+    def mm(o, l, x, start, stop):
+        op("P", lambda: g.tensor.matmul(out=ap(o), lhsT=ap(l), rhs=ap(x), start=start, stop=stop), [l, x], [o])
+
+    def dma(eng, out, in_, reads, writes, grp):
+        op(eng, lambda: Q[eng].dma_start(out=out, in_=in_), reads, writes, grp)
+
+    def iota(o, pattern, cm, base=0):
+        op("G", lambda: g.iota(ap(o), pattern, base, cm, allow_small_or_imprecise_dtypes=True), [], [o])
+
+    def sel(o, a, pattern, cmp, base, cm):
+        op("G", lambda: g.affine_select(ap(o), ap(a), pattern, cmp, 0.0, base, cm), [a], [o])
+
+    def Z(name, k):
+        return r(name, 15 - k, 143 - k)
+
+    dma("Y", T["AC"][:], T["an"][:], [], [r("AC")], "lAC")
+    dma("S", T["X2"][:, 0:TW], T["xc"][:], [], [r("X2", 0, TW)], "lX")
+    dma("Y", T["OC"][:], T["rf"][0::16, :], [], [r("OC")], "lOC")
+    dma("Y", T["wI"][:], T["w"][:], [], [r("wI")], "lWT")
+    dma("Y", T["thI"][:], T["th"][:], [], [r("thI")], "lWT")
+    dma("S", T["X2"][:, TW:2 * TW], T["xc"][:], [], [r("X2", TW, 2 * TW)], "lXb")
+    dma("Y", T["R"][:, 0:TW], T["rf"][:], [], [r("R", 0, TW)], "lR")
+
+    iota(r("pI"), [[1, 1]], 1)
+    iota(r("CB"), [[16, 8], [0, 16]], 0)
+    iota(r("CI"), [[1, 144]], 0)
+    iota(r("C16"), [[16, 16]], 0)
+    for name, c in (("ON", 1), ("CSO", -3 * (1 << 16)), ("CSE", -(1 << 17)), ("ONF", 1)):
+        iota(r(name), [[0, SCRATCH[name][1][1]]], 0, c)
+    cp(r("pF"), r("pI"))
+    ts(r("qI"), r("pI"), 112, OP.bitwise_and)
+    ts(r("rI"), r("pI"), 15, OP.bitwise_and)
+    ts(r("hI"), r("pI"), 4, OP.arith_shift_right, 1, OP.bitwise_and)
+    cp(r("q16"), r("qI"))
+    cp(r("rF"), r("rI"))
+    cp(r("m1"), r("hI"))
+    ts(r("c15"), r("qI"), 15.0, OP.add)
+    CI, C128 = r("CI"), r("CI", 0, 128)
+    ts(r("BON"), r("CB"), r("q16"), OP.is_equal, -4096.0, OP.mult)
+    sel(r("BON"), r("BON"), [[0, 8], [-1, 16]], OP.is_ge, KV - 1, 0)
+    O8 = r("ONF", 0, 128)
+    sel(r("IZ"), O8, [[-1, 128]], OP.is_equal, 0, 1)
+    sel(r("IZ"), r("IZ"), [[0, 8], [1, 16]], OP.not_equal, 0, 0)
+    sel(r("B0"), O8, [[-16, 8], [0, 16]], OP.is_equal, 0, 1)
+    sel(r("I0"), O8, [[-16, 8], [-1000, 16]], OP.is_equal, 0, 1)
+    sel(r("IDF"), O8, [[-1, 128]], OP.is_equal, 0, 1)
+    ts(r("m0"), r("m1"), 0.0, OP.is_equal)
+    ts(r("kI", 0, 1), r("rI"), 613.0, OP.mult)
+    ts(r("vtw"), r("C16"), r("rF"), OP.add)
+    ts(r("kI", 1, 2), r("kI", 0, 1), 2047, OP.bitwise_and)
+    for c in range(4):
+        ts(r("jc", c, c + 1), r("rF"), 16.0 * c + 0.5, OP.add)
+    ts(r("vw"), r("vtw"), 8.0, OP.mult)
+    cp(r("ck"), r("kI", 1, 2))
+    ts(r("AL", 16, 32), r("vtw"), float(TW), OP.add)
+    cp(r("OCF"), r("OC"))
+    cp(r("ACF"), r("AC"))
+    cp(r("wF"), r("wI"))
+    for s in range(4):
+        for h in range(2):
+            act(r("TI", 32 + 32 * s + 16 * h, 48 + 32 * s + 16 * h), r("OCF", s, 128, 8))
+    ts(r("ZW"), CI, r("c15"), OP.is_equal, r("wF"), OP.mult)
+    ts(r("BOW"), r("CB"), r("q16"), OP.is_equal, r("wF"), OP.mult)
+    for h in range(2):
+        act(r("TI", 16 * h, 16 * h + 16), r("ACF", 0, 128, 8))
+    ts(r("ID"), C128, r("pF"), OP.is_equal)
+    op("V", lambda: g.vector.transpose(out=ap(r("TT")), in_=ap(r("TI"))), [r("TI")], [r("TT")])
+    ts(r("NI"), C128, r("pF"), OP.is_equal, -1.0, OP.mult)
+    for n in range(5):
+        sl = (16 * n, 16 * n + 16)
+        act(r("t0", *sl), r("TT", 32 * n, 32 * n + 16), AF.Copy, scale=r("m0"))
+        ts(r("t1", *sl), r("TT", 32 * n + 16, 32 * n + 32), r("m1"), OP.mult)
+    tt(r("WW"), r("t0"), r("t1"), OP.add)
+    ts(r("Z4"), CI, r("c15"), OP.is_equal, 4096.0, OP.mult)
+    cp(r("AL", 0, 16), r("WW", 0, 16))
+    for p in range(16):
+        dma("Y", T["OWB"][p::16, :], T["OCF"][:], [r("OCF")], [r("OWB")], "gOW")
+    for p in range(16):
+        dma("Y", T["AA"][p::16, 0:TW], T["ACF"][:], [r("ACF")], [r("AA", 0, TW)], "gAA")
+    for k in range(16):
+        sel(r("E", k, 2048, 16), r("NI"), [[0, 128]], OP.is_equal, 0, 0)
+    sel(r("Z0F"), r("ONF"), [[16, 9], [1000, 16]], OP.is_equal, -15000, -1)
+    for o in ("BO", "Z1"):
+        w, x = (128, 0) if o == "BO" else (144, 1000)
+        sel(r(o), r("ON", 0, w), [[-16, w // 16], [x, 16]], OP.is_ge, -15 * x, 1)
+        sel(r(o), r(o), [[16, w // 16], [0, 16]], OP.is_ge, 15, -1)
+    iota(r("IOT"), [[1, 2048]], 0)
+
+    def uw_p(s):
+        for p in range(16):
+            mm(r("pW", 64 + 16 * s, 80 + 16 * s), Z("ZW", p), r("X2", 8 * p + s, TW, 128), p == 0, p == 15)
+
+    def lists(lo, hi):
+        a, b = 16 * lo, 16 * hi
+        cp(r("uwI", a, b), r("pW", 64 + a, 64 + b))
+        ts(r("uwA", a, b), r("uwI", a, b), 4095, OP.bitwise_and)
+        ts(r("uwF", a, b), r("uwA", a, b), 32.0, OP.add)
+        tt(r("pr", a, b), r("uwF", a, b), r("WW", 16 + a, 16 + b), OP.mult)
+        ts(r("bs", a, b), r("pr", a, b), 5, OP.arith_shift_right, 2047, OP.bitwise_and)
+        for k in list(range(KV, 16)) + list(range(KV)):
+            ts(r("OL", 64 * k + a, 64 * k + b), r("bs", a, b), float(613 * k % TW), OP.add)
+
+    def utab_p(s):
+        mm(r("pC", 0, 256), r("BOW"), r("X2", s, TW, 8), True, True)
+
+    def utab_v(s):
+        cp(r("uI"), r("pC", 0, 256))
+        ts(r("uA"), r("uI"), 4095, OP.bitwise_and)
+        ts(r("U", 256 * s, 256 * s + 256), r("uA"), 32.0, OP.add)
+
+    def qs(s):
+        act(r("QS", 256 * s, 256 * s + 256), r("X2", s, TW, 8))
+
+    def own_v(s, ks):
+        for k in ks:
+            tt(r("MX", 256 * k, 256 * k + 256), (r("X2"), r("OL", 64 * k + 16 * s, 64 * k + 16 * s + 16)),
+               r("QS", 256 * s, 256 * s + 256), OP.max)
+
+    SA, SB = list(range(KV, KV + KA)), list(range(KV + KA, 16))
+
+    def own_sg(s, ks):
+        for k in ks:
+            act(r("XG", 256 * (k - KV), 256 * (k - KV) + 256), (r("X2"), r("OL", 64 * k + 16 * s, 64 * k + 16 * s + 16)))
+
+    def own_sd(s, ks):
+        for k in ks[::2]:
+            b = "pD%d" % (k // 2 % 2)
+            mm(r(b), r("ID"), r("XG", 256 * (k - KV), 256 * (k - KV) + 512), True, False)
+            for h in range(2):
+                mm(r(b, 256 * h, 256 * h + 256), r("NI"), r("QS", 256 * s, 256 * s + 256), False, h == 1)
+
+    def own_sa(ks):
+        for k in ks[::2]:
+            act(r("MX", 256 * k, 256 * k + 512), r("pD%d" % (k // 2 % 2)), AF.Abs)
+
+    def own_p(s, ks, first=False, last=False):
+        o = r("pO", 0, 256)
+        if first:
+            mm(o, r("CSO"), r("ON"), True, False)
+            mm(o, r("BON"), r("QS", 256 * s, 256 * s + 256), False, False)
+        ks = list(ks)
+        for k in ks:
+            mm(o, Z("Z8" if k < KV else "Z4", k), r("MX", 256 * k, 256 * k + 256), False, last and k == ks[-1])
+
+    def own_w(s):
+        tt(r("wsx"), (r("SXS"), r("OL", 16 * s, 16 * s + 16)), r("OWB", s, TW, 8), OP.add)
+
+    def own_k(s):
+        tt(r("KN", 256 * s, 256 * s + 256), r("wsx"), r("pO", 0, 256), OP.add)
+
+    def wrap():
+        for p in range(16):
+            mm(r("pW", 0, 32), Z("Z0F", p), r("AB", p, 512, 16), p == 0, p == 15)
+
+    HALVES = sorted({x[1] // 128 for x in PLAN if x[0] == "D"})
+    NQ = sum(x[2] - x[1] for x in PLAN if x[0] == "Vq")
+
+    def turn(q):
+        for h in HALVES:
+            src = (q[0], q[1] + 128 * h, q[1] + 128 * h + 128, 1)
+            op("P", lambda: g.tensor.transpose(out=ap(r("pT", 128 * h, 128 * h + 128)), in_=ap(src), identity=ap(r("ID"))),
+               [src, r("ID")], [r("pT", 128 * h, 128 * h + 128)])
+        a, b = 128 * HALVES[0], 128 * HALVES[-1] + 128
+        act(r("QT", a, b), r("pT", a, b))
+
+    def spread(q, ng):
+        src = (q[0], q[1], q[1] + NQ, 1)
+        for k in range(16):
+            if k < 16 - ng:
+                act(r("QX", k, 16 * NQ, 16), src)
+            else:
+                sel(r("QX", k, 16 * NQ, 16), src, [[0, NQ]], OP.is_equal, 0, 0)
+
+    uw_p(0)
+    utab_p(0)
+    qs(0)
+    lists(0, 1)
+    utab_v(0)
+    turn(r("QS", 0, 256))
+    spread(r("QS", 0, 256), 0)
+    for c in range(4):
+        b = "pD%d" % (c % 2)
+        mm(r(b), r("BON"), r("X2", 512 * c, 512 * c + 512), True, True)
+        act(r("SXF", 512 * c, 512 * c + 512), r(b), AF.Identity, bias=float(4096 * 2048 + 2048))
+    dma("Y", T["SXF"][:, TW:2 * TW], T["SXF"][:, 0:TW], [r("SXF", 0, TW)], [r("SXF", TW, 2 * TW)], "gSF")
+    for k in range(16):
+        d = 613 * k % TW
+        dma("Y", T["SXS"][k::16, :], T["SXF"][k::16, d:d + TW], [r("SXF")], [r("SXS")], "gSX")
+    own_v(0, range(0, W0))
+    for s in range(1, 4):
+        uw_p(s)
+
+    for t in range(4):
+        if t == 0:
+            u, kn, ow = r("U", 0, 256), r("KN", 0, 256), r("OWB", 0, TW, 8)
+        else:
+            u, kn, ow = r("pE", 0, 256), r("pW", 128, 384), r("ow")
+            a, b = 64 * (t - 1), 64 * t
+            Q["V"].wait_ge(T.sem["arr%d" % (t - 1)], len(topo.engines(T.cores[(rank - t) % N], core)))
+            tt(r("bt"), r("ARR", a, b), r("R", 4 + t - 1, TW, 32), OP.max)
+            ts(r("R", 4 + t - 1, TW, 32), r("bt"), 2047, OP.bitwise_and)
+        cp(r("e"), (r("R", 0, TW), r("AL", 0, 16)))
+        tt(r("prod"), r("e"), u, OP.mult)
+        ts(r("pl"), r("prod"), 5, OP.arith_shift_right, 2047, OP.bitwise_and)
+        ts(r("pl16"), r("pl"), r("ck"), OP.add)
+        if t < 3:
+            utab_p(t + 1)
+        Ke = r("pK", 0, 256)
+        mm(Ke, r("CSE"), r("ON"), True, False)
+        mm(Ke, r("I0"), ow, False, False)
+        mm(Ke, r("IZ"), r("e"), False, False)
+        mm(r("pE", 0, 256), r("B0"), r("e"), True, True)
+        lastm = [x for x in PLAN if x[0] == "M"][-1]
+        for x in PLAN:
+            if x[0] == "Vq":
+                lo, hi = x[1:]
+                tt(r("DD", 16 * lo, 16 * hi), (r("X2"), r("pl16", lo, hi)), r("QX", 16 * lo, 16 * hi), OP.subtract)
+            elif x[0] == "Vg":
+                lo, hi = x[1:]
+                cp(r("XG", 16 * lo, 16 * hi), (r("X2"), r("pl16", lo, hi)))
+            elif x[0] == "Sg":
+                lo, hi = x[1:]
+                act(r("XG", 16 * lo, 16 * hi), (r("X2"), r("pl16", lo, hi)))
+            elif x[0] == "Q":
+                lo, hi = x[1:]
+                act(r("AD", 16 * lo, 16 * hi), r("DD", 16 * lo, 16 * hi), AF.Abs)
+            elif x[0] == "D":
+                lo, b, h = x[1], "pD%d" % x[2], x[1] // 128
+                mm(r(b), r("ID"), r("XG", 16 * lo, 16 * lo + 512), True, False)
+                mm(r(b), r("QT", 128 * h, 128 * h + 128), r("E", 16 * (lo - 128 * h), 16 * (lo - 128 * h) + 512), False, True)
+            elif x[0] == "A":
+                act(r("AD", 16 * x[1], 16 * x[1] + 512), r("pD%d" % x[2]), AF.Abs)
+            elif x[0] == "M":
+                lo, hi = x[1:]
+                for k in range(16):
+                    mm(r("pK", lo, hi), Z("Z4", k), r("AD", 16 * lo + k, 16 * hi, 16), False, x is lastm and k == 15)
+            elif t > 0:
+                own_w(t)
+                own_k(t)
+                act(r("kn"), (r("KN", 0, 256 * (t + 1)), r("VT16")))
+                mm(kn, r("IDF"), r("kn"), True, True)
+        if t == 0:
+            ts(r("Z8"), CI, r("c15"), OP.is_equal, 8192.0, OP.mult)
+            op("V", lambda: g.vector.memset(ap(r("F", 256, 264)), -4096), [], [r("F", 256, 264)])
+            ts(r("th4"), r("thI"), 4096.0, OP.mult, -float(1 << 24), OP.add)
+            own_v(0, range(W0, KV))
+            act(r("AA", TW, TW + 256), r("AA", 1, TW, 8))
+            act(r("AB"), (r("AA", 0, TW + 256), r("AL")))
+            wrap()
+            own_sg(0, SA + SB)
+            own_p(0, range(KV), True)
+            own_sd(0, SA + SB)
+            own_sa(SA + SB)
+            own_p(0, SA + SB, False, True)
+        if t < 3:
+            utab_v(t + 1)
+        tt(r("eqs"), r("e"), r("pE", 0, 256), OP.is_equal)
+        if t == 0:
+            own_w(0)
+            lists(1, 4)
+            own_k(0)
+            for s in range(1, 4):
+                qs(s)
+                act(r("AA", TW + 256 * s, TW + 256 * s + 256), r("AA", s + 1, TW, 8))
+            act(r("aB"), (r("IOT"), r("AL", 0, 16)))
+        tt(r("xk"), r("eqs"), kn, OP.mult)
+        cp(r("Aw"), r("pW", 0, 32))
+        tt(r("dA"), r("Aw", 16, 32), r("Aw", 0, 16), OP.subtract)
+        n1 = N1[t]
+        if t < 3:
+            own_v(t + 1, range(0, n1))
+            own_sg(t + 1, SA)
+        tt(r("m"), r("xk"), Ke, OP.min)
+        ts(r("hit"), r("m"), r("th4") if t == 0 else r("thb"), OP.is_lt)
+        mm(r("pC", 0, 256), r("BO"), r("hit"), True, True)
+        cw = r("pE", 256, 272)
+        for p in range(16):
+            mm(cw, Z("Z1", p), r("hit", p, 256, 16), p == 0, p == 15)
+        ts(r("F", 0, 256), r("m"), 2047, OP.bitwise_and)
+        ts(r("fitb"), r("pC", 0, 256), 7.5, OP.is_ge)
+        op("V", lambda: g.vector.tensor_tensor_scan(ap(r("cum")), ap(r("fitb")), ap(r("fitb")), 0.0, OP.add, OP.max),
+           [r("fitb")], [r("cum")])
+        for c in range(4):
+            act(r("junk", 256 * c, 256 * c + 256), r("cum"), AF.Sign, bias=r("jc", c, c + 1), scale=-1.0, acc=r("acc", c, c + 1))
+        ts(r("fit"), cw, 7.5, OP.is_ge)
+        ts(r("nf"), cw, 7.5, OP.is_lt, float(DUMP), OP.mult)
+        if t < 3:
+            ts(r("f256"), cw, 7.5, OP.is_ge, 256.0, OP.mult)
+        tt(r("tA"), r("fit"), r("dA"), OP.mult)
+        tt(r("vsw"), r("vw"), r("nf"), OP.add)
+        if t < 3:
+            tt(r("vtw"), r("vtw"), r("f256"), OP.add)
+        tt(r("aw"), r("tA"), r("Aw", 0, 16), OP.add)
+        tt(r("vw"), r("vw"), r("fit"), OP.add)
+        if t < 3:
+            cp(r("VT16"), r("vtw"))
+            ts(r("AL", 16, 32), r("vtw"), float(TW), OP.add)
+        cp(r("AL", 0, 16), r("aw"))
+        cp(r("VS16"), r("vsw"))
+        if t < 3:
+            own_sd(t + 1, SA)
+            own_sa(SA)
+            own_v(t + 1, range(n1, n1 + W1))
+        else:
+            scatter(r("AA"), r("VS16"), r("aB"))
+        ts(r("inv16", 0, 4), r("acc"), 0.5, OP.mult, 128.0, OP.add)
+        snd = r("SND", 64 * t, 64 * t + 64)
+        ts(snd, (r("F"), r("inv16", 0, 4)), 4096.0, OP.add)
+        dst = T.cores[(rank + 1 + t % (N - 1)) % N]
+        rid, pid = topo.addr(dst, core)
+        last = log["SND"][-1]
+        learn("G", "V", last[4], last[5])
+        g.remote_dma(ap(r("ARR", 64 * t, 64 * t + 64)), ap(snd), T.sem["arr%d" % t], T.sem["snd"], pid, rid, topo.mask(core, dst))
+        if t < 3:
+            mm(r("pE", 288, 304), r("ONF", 0, 128), r("fit"), True, True)
+            scatter(r("AA"), r("VS16"), r("aB"))
+            op("V", lambda: g.vector.tensor_reduce(ap(r("bsum")), ap(r("pE", 288, 304)), AxisListType.X, OP.add),
+               [r("pE", 288, 304)], [r("bsum")])
+        scatter(r("R"), r("VS16"), r("F", 0, 256))
+        if t < 3:
+            s, n = t + 1, 256 * (t + 2)
+            act(r("q"), (r("QS", 0, n), r("VT16")))
+            turn(r("q"))
+            act(r("u"), (r("U", 0, n), r("VT16")))
+            mm(r("pE", 0, 256), r("IDF"), r("u"), True, True)
+            if t == 0:
+                for c in range(4):
+                    act(r("OWN", 256 * c, 256 * c + 256), r("OWB", c, TW, 8))
+            act(r("AB"), (r("AA", 0, TW + n), r("AL")))
+            own_p(s, list(range(0, n1 + W1)) + SA, True)
+            spread(r("q"), NG)
+            own_sg(s, SB)
+            own_sd(s, SB)
+            wrap()
+            act(r("ow"), (r("OWN", 0, n), r("VT16")))
+            own_sa(SB)
+            act(r("aB"), (r("IOT"), r("AL", 0, 16)))
+            own_v(s, range(n1 + W1, n1 + W1 + 1))
+            cp(r("bI", 0, 1), r("bsum"))
+            own_v(s, range(n1 + W1 + 1, n1 + W1 + 2))
+            ts(r("bI", 1, 2), r("bI", 0, 1), 255, OP.bitwise_and)
+            own_v(s, range(n1 + W1 + 2, KV))
+            ts(r("thb"), r("bI", 1, 2), 4096.0, OP.mult, r("th4"), OP.add)
+            own_p(s, SB + list(range(n1 + W1, KV)), False, True)
+
+    cp(r("VT16"), r("vw"))
+    for s in range(4):
+        act(r("YA", s, 1024, 4), r("AA", s, TW, 8))
+    dma("Y", T["yan"][:], T["YA"][0::16, :], [r("YA")], [], "oA")
+    for s in range(2):
+        ts(r("junk", 256 * s, 256 * s + 256), r("R", 2 + s, TW, 8), 4096.0, OP.mult)
+    for s in range(2):
+        tt(r("YR", s, 512, 2), r("junk", 256 * s, 256 * s + 256), r("R", s, TW, 8), OP.add)
+    dma("Y", T["yr"][:], T["YR"][:], [r("YR")], [], "oR")
+    act(r("YL"), (r("IOT"), r("AL", 0, 16)))
+    act(r("YV"), (r("IOT"), r("VT16")))
+    dma("Y", T["ya"][:], T["YL"][0::16, :], [r("YL")], [], "oL")
+    dma("Y", T["yv"][:], T["YV"][0::16, :], [r("YV")], [], "oV")
+    for t in range(3):
+        cp(r("YH", t, 256, 4), r("R", 4 + t, TW, 32))
+    Q["V"].wait_ge(T.sem["arr3"], len(topo.engines(T.cores[(rank - 4) % N], core)))
+    tt(r("bt"), r("ARR", 192, 256), r("R", 7, TW, 32), OP.max)
+    ts(r("R", 7, TW, 32), r("bt"), 2047, OP.bitwise_and)
+    cp(r("YH", 3, 256, 4), r("R", 7, TW, 32))
+    dma("Y", T["yh"][:], T["YH"][:], [r("YH")], [], "oH")
+    for grp in DMAS:
+        g.wait_ge(T.sem[grp], 16 * DMAS[grp])
+    for e in "VSPG":
+        g.wait_ge(T.sem[e], count[e])
+    g.wait_ge(T.sem["snd"], sum(len(topo.engines(core, T.cores[(rank + 1 + t) % N])) for t in range(4)))

@@ -1,59 +1,48 @@
-from concourse.mybir import AluOpType as OP, ActivationFunctionType as AF, AxisListType
+from concourse.mybir import AluOpType as OP, ActivationFunctionType as AF
 
 TW = 2048
-DUMP = 3072
-KV = 12
-KA = 4
-N1 = (0, 4, 4, 0)
-W1 = 1
-W0 = 0
+BIG = float(1 << 25)
+KV = 10
 NG = 10
-PLAN = (("Vq", 0, 64), ("Vq", 64, 128), ("Vg", 128, 160), ("Sg", 192, 256), ("Q", 0, 64), ("Sg", 160, 192),
-        ("D", 192, 0), ("D", 224, 1), ("A", 192, 0), ("A", 224, 1), ("M", 0, 64), ("D", 128, 0), ("K",), ("D", 160, 1),
-        ("Q", 64, 128), ("M", 192, 256), ("A", 128, 0), ("A", 160, 1), ("M", 64, 128), ("M", 128, 192))
+XB = "SV"
+ES = "V"
+PLAN = ((128, 160, "S", "P"), (160, 192, "S", "P"), (192, 224, "S", "P"), (224, 256, "V", "P"), (0, 64, "V", "V"), (64, 128, "V", "V"))
+SUMS = ((128, 192), (192, 256), (0, 64), (64, 128))
+CYC, GATHER, SCATTER, PEC, HOP, DFIX, DBW, FLIGHT = 0.00083, 1.5, 3.5, 0.00042, 0.11, 0.9, 350e3, 1.7
 SCRATCH = {}
 for _n, _w, _d in (
-    ("X2", 4096, "bfloat16"), ("R", 5120, "int32"), ("AA", 5120, "float32"), ("OWB", 2048, "float32"),
-    ("OWN", 1024, "float32"), ("U", 1024, "float32"), ("KN", 1024, "float32"), ("QS", 1024, "bfloat16"),
-    ("IOT", 2048, "float32"), ("SXF", 4096, "float32"), ("SXS", 2048, "float32"), ("MX", 4096, "bfloat16"),
-    ("QX", 2048, "bfloat16"), ("XG", 4096, "bfloat16"), ("DD", 4096, "bfloat16"), ("AD", 4096, "bfloat16"),
-    ("E", 2048, "bfloat16"), ("q", 256, "bfloat16"), ("u", 256, "float32"), ("kn", 256, "float32"),
-    ("ow", 256, "float32"), ("aB", 256, "float32"), ("AB", 512, "float32"), ("e", 256, "float32"),
-    ("prod", 256, "int32"), ("pl", 256, "int32"), ("pl16", 256, "uint16"), ("eqs", 256, "float32"),
-    ("xk", 256, "float32"), ("m", 256, "int32"), ("hit", 256, "bfloat16"), ("F", 264, "int32"),
-    ("fitb", 256, "float32"), ("cum", 256, "float32"), ("junk", 1024, "float32"), ("acc", 4, "float32"),
-    ("inv16", 8, "uint16"), ("QT", 256, "bfloat16"), ("wsx", 256, "float32"),
-    ("fit", 16, "float32"), ("nf", 16, "float32"), ("f256", 16, "float32"), ("Aw", 32, "float32"), ("dA", 16, "float32"),
-    ("tA", 16, "float32"), ("aw", 16, "float32"), ("vtw", 16, "float32"), ("vw", 16, "float32"), ("vsw", 16, "float32"),
-    ("AL", 32, "uint16"), ("VT16", 16, "uint16"), ("VS16", 16, "uint16"),
-    ("bsum", 1, "float32"), ("bI", 2, "int32"), ("th4", 1, "float32"), ("thb", 1, "float32"),
-    ("thI", 1, "int32"), ("wI", 1, "int32"), ("wF", 1, "float32"),
-    ("pI", 1, "int32"), ("pF", 1, "float32"), ("qI", 1, "int32"), ("q16", 1, "float32"), ("c15", 1, "float32"),
-    ("rI", 1, "int32"), ("rF", 1, "float32"), ("hI", 1, "int32"), ("m1", 1, "float32"), ("m0", 1, "float32"),
-    ("kI", 2, "int32"), ("ck", 1, "float32"),
-    ("jc", 4, "float32"), ("CI", 144, "float32"), ("CB", 128, "float32"), ("C16", 16, "float32"),
-    ("Z1", 144, "bfloat16"), ("Z4", 144, "bfloat16"), ("Z8", 144, "bfloat16"), ("ZW", 144, "bfloat16"), ("Z0F", 144, "float32"),
-    ("BO", 128, "bfloat16"), ("BOW", 128, "bfloat16"), ("BON", 128, "bfloat16"), ("B0", 128, "float32"),
-    ("ID", 128, "bfloat16"), ("NI", 128, "bfloat16"), ("IZ", 128, "float32"), ("I0", 128, "float32"),
-    ("IDF", 128, "float32"), ("ONF", 144, "float32"),
-    ("ON", 256, "bfloat16"), ("CSE", 128, "bfloat16"), ("CSO", 128, "bfloat16"),
-    ("AC", 128, "int32"), ("OC", 128, "int32"), ("ACF", 128, "float32"), ("OCF", 128, "float32"),
-    ("TI", 160, "float32"), ("TT", 160, "float32"), ("t0", 80, "float32"), ("t1", 80, "float32"), ("WW", 80, "float32"),
-    ("uI", 256, "int32"), ("uA", 256, "int32"), ("uwI", 64, "int32"), ("uwA", 64, "int32"), ("uwF", 64, "float32"),
-    ("pr", 64, "int32"), ("bs", 64, "int32"), ("OL", 1024, "uint16"), ("bt", 64, "int32"),
-    ("YR", 512, "float32"), ("YH", 256, "float32"), ("YA", 1024, "float32"),
-    ("YV", 256, "float32"), ("YL", 256, "float32"),
-    ("SND", 256, "int32"), ("ARR", 256, "int32"),
+    ("X2", 4096, "bfloat16"), ("R", 4096, "int32"), ("AA", 4096, "int32"), ("IOT", 2048, "int32"), ("SXS", 2048, "float32"),
+    ("KN", 1024, "float32"), ("QS", 1024, "bfloat16"), ("MX", 8192, "bfloat16"), ("XS", 4096, "bfloat16"),
+    ("QX", 4096, "bfloat16"), ("XG", 4096, "bfloat16"), ("DD", 4096, "bfloat16"), ("AD", 4096, "bfloat16"),
+    ("SND", 4608, "int32"), ("ARR", 256, "int32"), ("OL", 1024, "uint16"), ("sx", 256, "float16"),
+    ("q", 256, "bfloat16"), ("QT", 256, "bfloat16"), ("AB", 512, "float16"), ("aB", 256, "float32"), ("e", 256, "float16"),
+    ("prod", 256, "int32"), ("pl", 256, "int32"), ("pl16", 256, "uint16"), ("pen", 256, "float32"), ("xk", 256, "float32"),
+    ("m", 256, "int32"), ("hit", 256, "bfloat16"), ("F", 256, "int32"),
+    ("fit", 16, "float32"), ("cum", 16, "bfloat16"), ("top", 16, "float32"), ("pos", 16, "uint16"), ("nf", 16, "float32"),
+    ("vs", 16, "float32"), ("VS", 16, "uint16"), ("Aw", 32, "float32"), ("dA", 16, "float32"), ("tA", 16, "float32"),
+    ("W", 48, "float32"), ("AL", 64, "uint16"), ("bI", 2, "int32"), ("th4", 1, "float32"), ("thb", 1, "float32"),
+    ("bt", 64, "int32"), ("b3", 64, "int32"), ("thI", 1, "int32"), ("wI", 1, "int32"), ("wF", 1, "float32"),
+    ("pI", 1, "int32"), ("pF", 1, "float32"), ("rI", 1, "int32"), ("rF", 1, "float32"), ("q16", 1, "float32"),
+    ("nr0", 1, "float32"), ("lu", 1, "float32"), ("kI", 2, "int32"), ("ck", 1, "float32"), ("OH", 16, "float32"),
+    ("CI", 144, "float32"), ("CB", 128, "float32"), ("C16", 16, "float32"), ("XI", 128, "int32"), ("XL", 64, "uint16"),
+    ("ci", 16, "bfloat16"), ("c32", 16, "bfloat16"), ("r32", 2, "int32"), ("p32", 1, "float32"), ("EI", 512, "bfloat16"),
+    ("E", 512, "bfloat16"), ("Z1", 144, "bfloat16"), ("Z4", 144, "bfloat16"), ("ZW", 144, "bfloat16"), ("ZA", 144, "bfloat16"),
+    ("BO", 128, "bfloat16"), ("BO2", 128, "bfloat16"), ("BQ", 128, "bfloat16"), ("LU", 128, "bfloat16"), ("LO", 128, "bfloat16"),
+    ("PD", 128, "bfloat16"), ("LT", 128, "bfloat16"), ("ID", 128, "bfloat16"), ("NI", 128, "bfloat16"), ("IZ", 128, "bfloat16"),
+    ("ON", 128, "bfloat16"), ("ZR", 128, "bfloat16"), ("N2", 128, "bfloat16"), ("ZN", 144, "bfloat16"),
+    ("AC", 128, "int32"), ("OC", 128, "int32"), ("uI", 128, "int32"), ("uA", 128, "int32"), ("uM", 128, "int32"),
+    ("u32", 128, "float32"), ("pr", 64, "int32"), ("bs", 64, "int32"), ("SXT", 128, "float32"),
+    ("YR", 512, "float32"), ("YH", 256, "float32"), ("YA", 1024, "float32"), ("YV", 16, "float32"),
 ):
     SCRATCH[_n] = ("sbuf", [128, _w], _d)
-PS = ("pK", "pE", "pO", "pD0", "pD1", "pC", "pW")
-for _n in PS:
+SCRATCH["SXD"] = ("dram", [8, 2 * TW], "float32")
+PSUM = ("pK", "pE", "pO", "pD0", "pD1", "pD2", "pC", "pW")
+for _n in PSUM:
     SCRATCH[_n] = ("psum", [128, 512], "float32")
-SCRATCH["pT"] = ("psum", [128, 1024], "bfloat16")
-PSUM = PS + ("pT",)
-DMAS = {"lAC": 1, "lOC": 1, "lWT": 2, "lX": 1, "lXb": 1, "lR": 1, "gOW": 16, "gAA": 16, "gSF": 1, "gSX": 16,
+DMAS = {"lAC": 1, "lOC": 1, "lW": 1, "lT": 1, "lX": 1, "lXb": 1, "lR": 1, "gAA": 3, "gSD": 2, "gSX": 16,
         "oR": 1, "oH": 1, "oA": 1, "oV": 1, "oL": 1}
 SEMAPHORES = ["V", "S", "P", "G", "snd"] + ["arr%d" % t for t in range(4)] + list(DMAS)
+_ORDER = []
 
 
 def _meet(a, b):
@@ -73,22 +62,58 @@ def _covers(a, b):
     return a == b or (a[2] == 1 and a[0] <= b[0] and a[1] >= b[1])
 
 
+def _place(busy, t, d):
+    for n, (a, b) in enumerate(busy):
+        if t + d <= a:
+            busy.insert(n, (t, t + d))
+            return t
+        t = max(t, b)
+    busy.append((t, t + d))
+    return t
+
+
+def _order(calls):
+    way = [0.0] * len(calls)
+    for i in range(len(calls) - 1, -1, -1):
+        c = calls[i]
+        way[i] += c["cost"] + c["late"]
+        for j in c["wait"]:
+            way[j] = max(way[j], way[i] + HOP)
+        for j in c["after"]:
+            way[j] = max(way[j], way[i] - calls[j]["late"])
+    busy = {k: [] for k in "VSPGYD"}
+    start, free, done = {}, {}, {}
+    for i in sorted(range(len(calls)), key=lambda i: (-way[i], i)):
+        c = calls[i]
+        t = max([0.0] + [done[j] + HOP for j in c["wait"]] + [free[j] for j in c["after"]])
+        start[i] = _place(busy[c["eng"]], t, c["cost"])
+        free[i] = done[i] = start[i] + c["cost"]
+        if c["ring"]:
+            done[i] = _place(busy["D"], free[i] + DFIX / 2, c["ring"]) + c["ring"] + DFIX / 2
+        elif c["late"]:
+            done[i] += c["late"]
+    return sorted(range(len(calls)), key=lambda i: (start[i], i))
+
+
 def rank_program(g, core, T, topo):
     rank = T.rank_of(core)
     if rank is None:
         return
     N = len(T.cores)
     Q = {"V": g.vector, "S": g.scalar, "P": g.tensor, "G": g, "Y": g.sync}
-    count = {k: 0 for k in "VSPG"}
-    known = {k: {} for k in Q}
-    log = {}
+    calls, log, groups, lastdma = [], {}, {}, {}
 
     def r(name, lo=0, hi=None, st=1):
         return (name, lo, SCRATCH[name][1][1] if hi is None else hi, st)
 
+    def rp(name, lo, hi, p0, p1):
+        return (name, lo, hi, 1, p0, p1)
+
     def ap(x):
         if len(x) == 2:
             return ap(x[0]).indirect(ap(x[1]))
+        if len(x) == 6:
+            return T[x[0]][x[4]:x[5], x[1]:x[2]]
         n, lo, hi, st = x
         return T[n][:, lo:hi:st] if st > 1 else T[n][:, lo:hi]
 
@@ -99,459 +124,384 @@ def rank_program(g, core, T, topo):
                 if len(x) == 2:
                     out += [x[0], x[1]]
                 else:
-                    out.append(x)
+                    out.append(x[:4])
         return out
 
-    def learn(eng, sem, val, clock):
-        kn = known[eng]
-        if kn.get(sem, 0) >= val:
-            return
-        Q[eng].wait_ge(T.sem[sem], val)
-        for s, x in clock.items():
-            if kn.get(s, 0) < x:
-                kn[s] = x
-        kn[sem] = max(kn.get(sem, 0), val)
+    def width(x):
+        return 16 * width(x[1]) if len(x) == 2 else -((x[1] - x[2]) // x[3])
 
-    def op(eng, fn, reads, writes, grp=None):
-        reads, writes = flat(reads), flat(writes)
-        need = {}
-        for acc, wr in [(x, False) for x in reads] + [(x, True) for x in writes]:
+    def short(*xs):
+        return all(SCRATCH[x[0]][2].endswith("16") for x in xs)
+
+    def op(eng, fn, reads, writes, cost, grp=None, late=0.0, ring=0.0, send=None):
+        me = len(calls)
+        uses = [(x, False) for x in flat(reads)] + [(x, True) for x in flat(writes)]
+        wait, after = {}, set()
+        for acc, wr in uses:
             bank = acc[0] in PSUM
-            for (sp, w2, eng2, sem, val, clock, grp2) in log.get(acc[0], ()):
-                if grp is not None and grp2 == grp:
+            for (sp, w2, j) in log.get(acc[0], ()):
+                c = calls[j]
+                if grp is not None and c["grp"] == grp:
                     continue
-                if eng2 == eng and grp2 is None and grp is None:
-                    if (bank and eng == "P") or not (wr or w2) or not _meet(acc[1:], sp):
-                        continue
-                elif bank:
-                    pass
-                else:
-                    if not (wr or w2) or not _meet(acc[1:], sp):
-                        continue
-                if sem not in need or need[sem][0] < val:
-                    need[sem] = (val, clock)
-        for sem in sorted(need, key=lambda s: -len(need[s][1])):
-            learn(eng, sem, need[sem][0], need[sem][1])
-        ins = fn()
-        if grp is None:
-            count[eng] += 1
-            sem, val = eng, count[eng]
-            ins.then_inc(T.sem[sem], 1)
-        else:
-            sem, val = grp, 16 * DMAS[grp]
-            ins.then_inc(T.sem[sem], 16)
-        clock = dict(known[eng])
-        clock[sem] = val
-        for acc, wr in [(x, False) for x in reads] + [(x, True) for x in writes]:
-            old = log.setdefault(acc[0], [])
-            keep = []
-            for rec in old:
-                gone = False
-                if grp is None or rec[6] != grp:
-                    if wr and _covers(acc[1:], rec[0]):
-                        gone = True
-                    elif not wr and not rec[1] and rec[2] == eng and rec[6] is None and grp is None and _covers(acc[1:], rec[0]):
-                        gone = True
-                if not gone:
-                    keep.append(rec)
-            keep.append((acc[1:], wr, eng, sem, val, clock, grp))
-            log[acc[0]] = keep
+                if bank and c["eng"] == eng == "P":
+                    after.add(j)
+                elif (bank and c["eng"] != eng) or ((wr or w2) and _meet(acc[1:], sp)):
+                    for k in groups.get(c["grp"], [j]):
+                        wait[k] = acc[0]
+        if ring or send is not None:
+            if eng in lastdma:
+                after.add(lastdma[eng])
+            lastdma[eng] = me
+        if grp is not None:
+            groups.setdefault(grp, []).append(me)
+        calls.append(dict(eng=eng, fn=fn, cost=cost, late=late + (ring and ring + DFIX), ring=ring, grp=grp, send=send, wait=wait, after=after))
+        for acc, wr in uses:
+            keep = [rec for rec in log.get(acc[0], ())
+                    if not (wr and _covers(acc[1:], rec[0]) and (grp is None or calls[rec[2]]["grp"] != grp))]
+            if acc[0] in PSUM and eng == "P":
+                keep = [rec for rec in keep if rec[2] not in wait and rec[2] not in after]
+            log[acc[0]] = keep + [(acc[1:], wr, me)]
+
+    def issue():
+        if not _ORDER:
+            _ORDER.extend(_order(calls))
+        count = {k: 0 for k in "VSPG"}
+        known = {k: {} for k in Q}
+        mark = {}
+        sent = 0
+        for i in _ORDER:
+            c = calls[i]
+            kn = known[c["eng"]]
+            need = [mark[j]["ARR" if calls[j]["send"] is not None and name == "ARR" else ""] for j, name in c["wait"].items()]
+            for sem, val, clock in sorted(need, key=lambda x: (-len(x[2]), -x[1])):
+                if kn.get(sem, 0) < val:
+                    Q[c["eng"]].wait_ge(T.sem[sem], val)
+                    for s, x in list(clock.items()) + [(sem, val)]:
+                        kn[s] = max(kn.get(s, 0), x)
+            ins = c["fn"]()
+            if c["send"] is not None:
+                out, inn = c["send"]
+                sent += out
+                mark[i] = {"": ("snd", sent, dict(kn)), "ARR": (inn[0], inn[1], {})}
+            elif c["grp"] is not None:
+                ins.then_inc(T.sem[c["grp"]], 16)
+                mark[i] = {"": (c["grp"], 16 * DMAS[c["grp"]], dict(kn))}
+            else:
+                count[c["eng"]] += 1
+                ins.then_inc(T.sem[c["eng"]], 1)
+                mark[i] = {"": (c["eng"], count[c["eng"]], dict(kn))}
+        for grp in groups:
+            g.wait_ge(T.sem[grp], 16 * DMAS[grp])
+        for e in "VSPG":
+            g.wait_ge(T.sem[e], count[e])
+        g.wait_ge(T.sem["snd"], sent)
 
     def sc(x):
         return ap(x) if isinstance(x, tuple) else x
 
+    def vcost(o, a, per):
+        if len(a) == 2:
+            return 0.05 + CYC * GATHER * width(a)
+        return 0.02 + CYC * max(64, per * width(a))
+
     def tt(o, a, b, f):
-        op("V", lambda: g.vector.tensor_tensor(out=ap(o), in0=ap(a), in1=ap(b), op=f), [a, b], [o])
+        per = 1 if a[0] in PSUM or b[0] in PSUM else 2
+        op("V", lambda: g.vector.tensor_tensor(out=ap(o), in0=ap(a), in1=ap(b), op=f), [a, b], [o], vcost(o, a, per))
 
     def ts(o, a, s1, f, s2=None, f2=None):
-        if f2 is None:
-            op("V", lambda: g.vector.tensor_scalar(out=ap(o), in0=ap(a), scalar1=sc(s1), scalar2=None, op0=f), [a, s1], [o])
-        else:
-            op("V", lambda: g.vector.tensor_scalar(out=ap(o), in0=ap(a), scalar1=sc(s1), scalar2=sc(s2), op0=f, op1=f2), [a, s1, s2], [o])
+        kw = {} if f2 is None else {"op1": f2}
+        op("V", lambda: g.vector.tensor_scalar(out=ap(o), in0=ap(a), scalar1=sc(s1), scalar2=sc(s2), op0=f, **kw), [a, s1, s2], [o],
+           vcost(o, a, 0.5 if short(o, a) else 1))
 
     def cp(o, a):
-        op("V", lambda: g.vector.tensor_copy(out=ap(o), in_=ap(a)), [a], [o])
+        op("V", lambda: g.vector.tensor_copy(out=ap(o), in_=ap(a)), [a], [o], vcost(o, a, 0.5 if len(a) > 2 and short(o, a) else 1))
 
     def scatter(win, off, a):
-        op("V", lambda: g.vector.tensor_copy(out=ap((win, off)), in_=ap(a)), [a, off], [win])
+        op("V", lambda: g.vector.tensor_copy(out=ap((win, off)), in_=ap(a)), [a, off], [win], 0.05 + CYC * SCATTER * width(a))
 
-    def act(o, a, f=AF.Copy, bias=None, scale=None, acc=None):
+    def act(o, a, f=AF.Copy, bias=None, scale=None):
         kw = {}
         if bias is not None:
             kw["bias"] = sc(bias)
         if scale is not None:
             kw["scale"] = sc(scale)
-        if acc is not None:
-            kw["accum_out"] = ap(acc)
-        op("S", lambda: g.scalar.activation(out=ap(o), in_=ap(a), func=f, **kw), [a, bias, scale], [o] + ([acc] if acc else []))
+        op("S", lambda: g.scalar.activation(out=ap(o), in_=ap(a), func=f, **kw), [a, bias, scale], [o],
+           0.06 + CYC * max(64, width(a) * (GATHER if len(a) == 2 else 1)))
+
+    def move(eng, o, a):
+        (cp if eng == "V" else act)(o, a)
 
     def mm(o, l, x, start, stop):
-        op("P", lambda: g.tensor.matmul(out=ap(o), lhsT=ap(l), rhs=ap(x), start=start, stop=stop), [l, x], [o])
+        op("P", lambda: g.tensor.matmul(out=ap(o), lhsT=ap(l), rhs=ap(x), start=start, stop=stop), [l, x], [o],
+           0.01 + PEC * max(64, width(x)))
 
-    def dma(eng, out, in_, reads, writes, grp):
-        op(eng, lambda: Q[eng].dma_start(out=out, in_=in_), reads, writes, grp)
+    def dma(eng, out, in_, reads, writes, grp, size):
+        op(eng, lambda: Q[eng].dma_start(out=out, in_=in_), reads, writes, 0.05, grp, ring=0.13 + size / DBW)
 
     def iota(o, pattern, cm, base=0):
-        op("G", lambda: g.iota(ap(o), pattern, base, cm, allow_small_or_imprecise_dtypes=True), [], [o])
+        op("G", lambda: g.iota(ap(o), pattern, base, cm, allow_small_or_imprecise_dtypes=True), [], [o], 0.13 + 2 * CYC * width(o))
 
-    def sel(o, a, pattern, cmp, base, cm):
-        op("G", lambda: g.affine_select(ap(o), ap(a), pattern, cmp, 0.0, base, cm), [a], [o])
+    def fill(o, c):
+        iota(o, [[0, o[2] - o[1]]], 0, c)
+
+    def sel(o, a, pattern, cmp, base, cm, other=0.0):
+        op("G", lambda: g.affine_select(ap(o), ap(a), pattern, cmp, other, base, cm), [a], [o], 0.17 + 2 * CYC * width(o))
 
     def Z(name, k):
         return r(name, 15 - k, 143 - k)
 
-    dma("Y", T["AC"][:], T["an"][:], [], [r("AC")], "lAC")
-    dma("S", T["X2"][:, 0:TW], T["xc"][:], [], [r("X2", 0, TW)], "lX")
-    dma("Y", T["OC"][:], T["rf"][0::16, :], [], [r("OC")], "lOC")
-    dma("Y", T["wI"][:], T["w"][:], [], [r("wI")], "lWT")
-    dma("Y", T["thI"][:], T["th"][:], [], [r("thI")], "lWT")
-    dma("S", T["X2"][:, TW:2 * TW], T["xc"][:], [], [r("X2", TW, 2 * TW)], "lXb")
-    dma("Y", T["R"][:, 0:TW], T["rf"][:], [], [r("R", 0, TW)], "lR")
+    def col(name, c):
+        return r(name, c, c + 1)
 
-    iota(r("pI"), [[1, 1]], 1)
-    iota(r("CB"), [[16, 8], [0, 16]], 0)
-    iota(r("CI"), [[1, 144]], 0)
-    iota(r("C16"), [[16, 16]], 0)
-    for name, c in (("ON", 1), ("CSO", -3 * (1 << 16)), ("CSE", -(1 << 17)), ("ONF", 1)):
-        iota(r(name), [[0, SCRATCH[name][1][1]]], 0, c)
-    cp(r("pF"), r("pI"))
-    ts(r("qI"), r("pI"), 112, OP.bitwise_and)
-    ts(r("rI"), r("pI"), 15, OP.bitwise_and)
-    ts(r("hI"), r("pI"), 4, OP.arith_shift_right, 1, OP.bitwise_and)
-    cp(r("q16"), r("qI"))
-    cp(r("rF"), r("rI"))
-    cp(r("m1"), r("hI"))
-    ts(r("c15"), r("qI"), 15.0, OP.add)
-    CI, C128 = r("CI"), r("CI", 0, 128)
-    ts(r("BON"), r("CB"), r("q16"), OP.is_equal, -4096.0, OP.mult)
-    sel(r("BON"), r("BON"), [[0, 8], [-1, 16]], OP.is_ge, KV - 1, 0)
-    O8 = r("ONF", 0, 128)
-    sel(r("IZ"), O8, [[-1, 128]], OP.is_equal, 0, 1)
-    sel(r("IZ"), r("IZ"), [[0, 8], [1, 16]], OP.not_equal, 0, 0)
-    sel(r("B0"), O8, [[-16, 8], [0, 16]], OP.is_equal, 0, 1)
-    sel(r("I0"), O8, [[-16, 8], [-1000, 16]], OP.is_equal, 0, 1)
-    sel(r("IDF"), O8, [[-1, 128]], OP.is_equal, 0, 1)
-    ts(r("m0"), r("m1"), 0.0, OP.is_equal)
-    ts(r("kI", 0, 1), r("rI"), 613.0, OP.mult)
-    ts(r("vtw"), r("C16"), r("rF"), OP.add)
-    ts(r("kI", 1, 2), r("kI", 0, 1), 2047, OP.bitwise_and)
-    for c in range(4):
-        ts(r("jc", c, c + 1), r("rF"), 16.0 * c + 0.5, OP.add)
-    ts(r("vw"), r("vtw"), 8.0, OP.mult)
-    cp(r("ck"), r("kI", 1, 2))
-    ts(r("AL", 16, 32), r("vtw"), float(TW), OP.add)
-    cp(r("OCF"), r("OC"))
-    cp(r("ACF"), r("AC"))
-    cp(r("wF"), r("wI"))
-    for s in range(4):
+    aL, v1L, vtL, v0L = (r("AL", 16 * n, 16 * n + 16) for n in range(4))
+    aw, v1, vt = (r("W", 16 * n, 16 * n + 16) for n in range(3))
+    MV = r("AB", 256, 512)
+    u, pd = r("pE", 0, 256), r("pE", 256, 512)
+    c2, off, tot = r("pC", 0, 16), col("pE", 256), col("pE", 257)
+    Ke = r("pK", 0, 256)
+    KB = 1024
+
+    dma("S", T["wI"][:], T["w"][:], [], [r("wI")], "lW", 512)
+    dma("S", T["X2"][:, 0:TW], T["xc"][:], [], [r("X2", 0, TW)], "lX", 512 * KB)
+    dma("Y", T["OC"][:], T["rf"][0::16, :], [], [r("OC")], "lOC", 64 * KB)
+    dma("Y", T["AC"][:], T["an"][:], [], [r("AC")], "lAC", 64 * KB)
+    if XB == "D":
+        dma("S", T["X2"][:, TW:2 * TW], T["xc"][:], [], [r("X2", TW, 2 * TW)], "lXb", 512 * KB)
+        dma("Y", T["thI"][:], T["th"][:], [], [r("thI")], "lT", 512)
+    else:
+        dma("S", T["thI"][:], T["th"][:], [], [r("thI")], "lT", 512)
         for h in range(2):
-            act(r("TI", 32 + 32 * s + 16 * h, 48 + 32 * s + 16 * h), r("OCF", s, 128, 8))
-    ts(r("ZW"), CI, r("c15"), OP.is_equal, r("wF"), OP.mult)
-    ts(r("BOW"), r("CB"), r("q16"), OP.is_equal, r("wF"), OP.mult)
-    for h in range(2):
-        act(r("TI", 16 * h, 16 * h + 16), r("ACF", 0, 128, 8))
+            move(XB[h], r("X2", TW + 1024 * h, TW + 1024 * h + 1024), r("X2", 1024 * h, 1024 * h + 1024))
+    dma("Y", T["R"][:, 0:TW], T["rf"][:], [], [r("R", 0, TW)], "lR", KB * KB)
+
+    op("V", lambda: g.vector.memset(ap(r("AA", 0, TW)), 1), [], [r("AA", 0, TW)], CYC * TW)
+    iota(r("pI"), [[1, 1]], 1)
+    iota(r("pF"), [[1, 1]], 1)
+    iota(r("CI"), [[1, 144]], 0)
+    iota(r("XI", 0, 64), [[1, 4], [8, 16]], 128)
+    iota(r("CB"), [[16, 8], [0, 16]], 0)
+    iota(r("C16"), [[16, 16]], 0)
+    iota(r("EI"), [[1, 32], [0, 16]], 0)
+    C128 = r("CI", 0, 128)
+    ts(r("rI"), r("pI"), 15, OP.bitwise_and)
+    ts(r("XI", 64, 128), r("XI", 0, 64), TW - 1, OP.bitwise_and)
+    cp(r("rF"), r("rI"))
+    cp(r("XL"), r("XI", 64, 128))
+    tt(r("q16"), r("pF"), r("rF"), OP.subtract)
+    act(r("wF"), r("wI"))
+    ts(col("r32", 0), r("pI"), 31, OP.bitwise_and)
+    ts(r("Z1"), r("CI"), -15.0, OP.add, r("q16"), OP.is_equal)
+    ts(r("OH"), r("CI", 0, 16), r("rF"), OP.is_equal)
+    act(r("ZW"), r("Z1"), AF.Copy, scale=r("wF"))
+    act(r("Z4"), r("Z1"), AF.Copy, scale=4096.0)
     ts(r("ID"), C128, r("pF"), OP.is_equal)
-    op("V", lambda: g.vector.transpose(out=ap(r("TT")), in_=ap(r("TI"))), [r("TI")], [r("TT")])
-    ts(r("NI"), C128, r("pF"), OP.is_equal, -1.0, OP.mult)
-    for n in range(5):
-        sl = (16 * n, 16 * n + 16)
-        act(r("t0", *sl), r("TT", 32 * n, 32 * n + 16), AF.Copy, scale=r("m0"))
-        ts(r("t1", *sl), r("TT", 32 * n + 16, 32 * n + 32), r("m1"), OP.mult)
-    tt(r("WW"), r("t0"), r("t1"), OP.add)
-    ts(r("Z4"), CI, r("c15"), OP.is_equal, 4096.0, OP.mult)
-    cp(r("AL", 0, 16), r("WW", 0, 16))
-    for p in range(16):
-        dma("Y", T["OWB"][p::16, :], T["OCF"][:], [r("OCF")], [r("OWB")], "gOW")
-    for p in range(16):
-        dma("Y", T["AA"][p::16, 0:TW], T["ACF"][:], [r("ACF")], [r("AA", 0, TW)], "gAA")
-    for k in range(16):
-        sel(r("E", k, 2048, 16), r("NI"), [[0, 128]], OP.is_equal, 0, 0)
-    sel(r("Z0F"), r("ONF"), [[16, 9], [1000, 16]], OP.is_equal, -15000, -1)
-    for o in ("BO", "Z1"):
-        w, x = (128, 0) if o == "BO" else (144, 1000)
-        sel(r(o), r("ON", 0, w), [[-16, w // 16], [x, 16]], OP.is_ge, -15 * x, 1)
-        sel(r(o), r(o), [[16, w // 16], [0, 16]], OP.is_ge, 15, -1)
-    iota(r("IOT"), [[1, 2048]], 0)
+    ts(r("BO"), r("CB"), r("q16"), OP.is_equal)
+    cp(r("p32"), col("r32", 0))
+    ts(v1, r("XI", 64, 80), 1.0, OP.add)
+    ts(vt, r("C16"), r("rF"), OP.add, 4.0, OP.mult)
+    ts(r("lu"), col("OH", 4), 2080.0, OP.mult, col("OH", 3), OP.add)
+    ts(r("nr0"), r("rF"), 0.0, OP.not_equal)
+    cp(r("AL", 16, 48), r("W", 16, 48))
+    cp(aL, r("AC", 0, 128, 8))
+    ts(col("kI", 0), r("rI"), 613.0, OP.mult)
+    ts(col("kI", 1), col("kI", 0), TW - 1, OP.bitwise_and)
+    cp(r("ck"), col("kI", 1))
+    ts(r("E"), r("EI"), r("p32"), OP.is_equal, -1.0, OP.mult)
+    ts(r("ci"), r("XI", 64, 80), 0.125, OP.mult, -256.0, OP.add)
+    ts(r("th4"), r("thI"), 4096.0, OP.mult, -float(1 << 24), OP.add)
+    if any(x[3] == "R" for x in PLAN):
+        act(r("ZN"), r("Z1"), AF.Copy, scale=-4096.0)
+    act(r("NI"), r("ID"), AF.Copy, scale=-1.0)
+    act(r("N2"), r("ID"), AF.Copy, scale=-2048.0)
+    act(r("LU"), r("BO"), AF.Copy, scale=r("lu"))
+    act(r("BO2"), r("BO"), AF.Copy, scale=col("OH", 2))
+    act(r("IZ"), r("ID"), AF.Copy, scale=r("nr0"))
+    act(r("ZA"), r("Z1"), AF.Copy, scale=col("OH", 0))
+    dma("Y", T["AA"][0::16, 0:TW], T["an"][:], [], [r("AA", 0, TW)], "gAA", 64 * KB)
+    dma("Y", T["AA"][2::16, 1:TW + 1], T["rf"][0::16, :], [], [r("AA", 1, TW + 1)], "gAA", 64 * KB)
+    fill(r("ZR"), 0)
+    fill(r("BQ"), -2048)
+    sel(r("BQ"), r("BQ"), [[0, 8], [-1, 16]], OP.is_ge, KV - 1, 0, 2048.0)
+    sel(r("BQ"), r("BQ"), [[-16, 8], [0, 16]], OP.is_ge, 0, 1)
+    sel(r("BQ"), r("BQ"), [[16, 8], [0, 16]], OP.is_ge, 15, -1)
+    sel(r("PD"), r("ZR"), [[-1, 128]], OP.not_equal, 0, 1, BIG)
+    sel(r("PD"), r("PD"), [[-16, 8], [0, 16]], OP.not_equal, 0, 1, -BIG)
+    sel(r("PD"), r("PD"), [[0, 8], [1, 16]], OP.not_equal, 0, 0)
+    sel(r("LO"), r("ZR"), [[-16, 8], [-1000, 16]], OP.not_equal, -2, 1, 1.0)
+    sel(r("LO"), r("LO"), [[-16, 8], [0, 16]], OP.not_equal, -4, 1, -float(1 << 24))
+    fill(r("ON"), 1)
+    fill(r("c32"), 32)
+    sel(r("LT"), r("BO"), [[1, 128]], OP.is_gt, 0, -1)
+    for h in range(4):
+        iota(r("IOT", 512 * h, 512 * h + 512), [[1, 512]], 0, 512 * h)
+    for h in range(2):
+        fill(r("KN", 512 * h, 512 * h + 512), 0)
+    fill(r("SND", 0, 256), 4096)
 
-    def uw_p(s):
-        for p in range(16):
-            mm(r("pW", 64 + 16 * s, 80 + 16 * s), Z("ZW", p), r("X2", 8 * p + s, TW, 128), p == 0, p == 15)
+    def ol(s, k):
+        return r("OL", 64 * k + 16 * s, 64 * k + 16 * s + 16)
 
-    def lists(lo, hi):
-        a, b = 16 * lo, 16 * hi
-        cp(r("uwI", a, b), r("pW", 64 + a, 64 + b))
-        ts(r("uwA", a, b), r("uwI", a, b), 4095, OP.bitwise_and)
-        ts(r("uwF", a, b), r("uwA", a, b), 32.0, OP.add)
-        tt(r("pr", a, b), r("uwF", a, b), r("WW", 16 + a, 16 + b), OP.mult)
-        ts(r("bs", a, b), r("pr", a, b), 5, OP.arith_shift_right, 2047, OP.bitwise_and)
-        for k in list(range(KV, 16)) + list(range(KV)):
-            ts(r("OL", 64 * k + a, 64 * k + b), r("bs", a, b), float(613 * k % TW), OP.add)
+    def own(s):
+        qs, o, m0 = r("QS", 256 * s, 256 * s + 256), r("pO", 0, 256), 4096 * (s % 2)
+        mm(o, r("BQ"), qs, True, False)
+        act(r("sx"), (r("SXS"), ol(s, 0)))
+        ks = [(k, 1) for k in range(KV)]
+        for n, k in enumerate(range(KV, 16, 2)):
+            ks.insert(min(len(ks), 2 * n + 1), (k, 2))
+        for k, n in ks:
+            mx = r("MX", m0 + 256 * k, m0 + 256 * (k + n))
+            if n == 1:
+                tt(mx, (r("X2"), ol(s, k)), qs, OP.max)
+            else:
+                for h in range(2):
+                    act(r("XS", 256 * (k + h), 256 * (k + h + 1)), (r("X2"), ol(s, k + h)))
+                mm(r("pD2"), r("ID"), r("XS", 256 * k, 256 * k + 512), True, False)
+                for h in range(2):
+                    mm(r("pD2", 256 * h, 256 * h + 256), r("NI"), qs, False, h == 1)
+                act(mx, r("pD2"), AF.Relu)
+            for h in range(n):
+                mm(o, Z("Z4", k + h), r("MX", m0 + 256 * (k + h), m0 + 256 * (k + h + 1)), False, False)
+        mm(o, r("N2"), r("sx"), False, True)
+        act(r("KN", s, 1024, 4), o, AF.Identity, bias=float(2048 - 3 * (1 << 23)), scale=2.0)
 
-    def utab_p(s):
-        mm(r("pC", 0, 256), r("BOW"), r("X2", s, TW, 8), True, True)
+    HALVES = sorted({x[0] // 128 for x in PLAN if x[3] == "P"})
+    NQ = sum(x[1] - x[0] for x in PLAN if x[3] != "P")
 
-    def utab_v(s):
-        cp(r("uI"), r("pC", 0, 256))
-        ts(r("uA"), r("uI"), 4095, OP.bitwise_and)
-        ts(r("U", 256 * s, 256 * s + 256), r("uA"), 32.0, OP.add)
-
-    def qs(s):
-        act(r("QS", 256 * s, 256 * s + 256), r("X2", s, TW, 8))
-
-    def own_v(s, ks):
-        for k in ks:
-            tt(r("MX", 256 * k, 256 * k + 256), (r("X2"), r("OL", 64 * k + 16 * s, 64 * k + 16 * s + 16)),
-               r("QS", 256 * s, 256 * s + 256), OP.max)
-
-    SA, SB = list(range(KV, KV + KA)), list(range(KV + KA, 16))
-
-    def own_sg(s, ks):
-        for k in ks:
-            act(r("XG", 256 * (k - KV), 256 * (k - KV) + 256), (r("X2"), r("OL", 64 * k + 16 * s, 64 * k + 16 * s + 16)))
-
-    def own_sd(s, ks):
-        for k in ks[::2]:
-            b = "pD%d" % (k // 2 % 2)
-            mm(r(b), r("ID"), r("XG", 256 * (k - KV), 256 * (k - KV) + 512), True, False)
-            for h in range(2):
-                mm(r(b, 256 * h, 256 * h + 256), r("NI"), r("QS", 256 * s, 256 * s + 256), False, h == 1)
-
-    def own_sa(ks):
-        for k in ks[::2]:
-            act(r("MX", 256 * k, 256 * k + 512), r("pD%d" % (k // 2 % 2)), AF.Abs)
-
-    def own_p(s, ks, first=False, last=False):
-        o = r("pO", 0, 256)
-        if first:
-            mm(o, r("CSO"), r("ON"), True, False)
-            mm(o, r("BON"), r("QS", 256 * s, 256 * s + 256), False, False)
-        ks = list(ks)
-        for k in ks:
-            mm(o, Z("Z8" if k < KV else "Z4", k), r("MX", 256 * k, 256 * k + 256), False, last and k == ks[-1])
-
-    def own_w(s):
-        tt(r("wsx"), (r("SXS"), r("OL", 16 * s, 16 * s + 16)), r("OWB", s, TW, 8), OP.add)
-
-    def own_k(s):
-        tt(r("KN", 256 * s, 256 * s + 256), r("wsx"), r("pO", 0, 256), OP.add)
-
-    def wrap():
-        for p in range(16):
-            mm(r("pW", 0, 32), Z("Z0F", p), r("AB", p, 512, 16), p == 0, p == 15)
-
-    HALVES = sorted({x[1] // 128 for x in PLAN if x[0] == "D"})
-    NQ = sum(x[2] - x[1] for x in PLAN if x[0] == "Vq")
-
-    def turn(q):
+    def ready(q, ng):
         for h in HALVES:
-            src = (q[0], q[1] + 128 * h, q[1] + 128 * h + 128, 1)
-            op("P", lambda: g.tensor.transpose(out=ap(r("pT", 128 * h, 128 * h + 128)), in_=ap(src), identity=ap(r("ID"))),
-               [src, r("ID")], [r("pT", 128 * h, 128 * h + 128)])
+            mm(r("pW", 128 + 128 * h, 256 + 128 * h), (q[0], q[1] + 128 * h, q[1] + 128 * h + 128, 1), r("ID"), True, True)
         a, b = 128 * HALVES[0], 128 * HALVES[-1] + 128
-        act(r("QT", a, b), r("pT", a, b))
-
-    def spread(q, ng):
+        act(r("QT", a, b), r("pW", 128 + a, 128 + b))
         src = (q[0], q[1], q[1] + NQ, 1)
-        for k in range(16):
+        for k in range(16 if NQ else 0):
             if k < 16 - ng:
                 act(r("QX", k, 16 * NQ, 16), src)
             else:
                 sel(r("QX", k, 16 * NQ, 16), src, [[0, NQ]], OP.is_equal, 0, 0)
+        act(MV, (r("AA", 0, TW), v1L))
+        mm(u, r("LU"), MV, True, True)
 
-    uw_p(0)
-    utab_p(0)
-    qs(0)
-    lists(0, 1)
-    utab_v(0)
-    turn(r("QS", 0, 256))
-    spread(r("QS", 0, 256), 0)
-    for c in range(4):
-        b = "pD%d" % (c % 2)
-        mm(r(b), r("BON"), r("X2", 512 * c, 512 * c + 512), True, True)
-        act(r("SXF", 512 * c, 512 * c + 512), r(b), AF.Identity, bias=float(4096 * 2048 + 2048))
-    dma("Y", T["SXF"][:, TW:2 * TW], T["SXF"][:, 0:TW], [r("SXF", 0, TW)], [r("SXF", TW, 2 * TW)], "gSF")
+    for p in range(16):
+        mm(r("pW", 0, 128), Z("ZW", p), r("X2", 128 * p, 128 * p + 128), p == 0, p == 15)
+    for p in range(16):
+        mm(r("pC", 0, 128), Z("Z1", p), r("X2", 128 * p, 128 * p + 128), p == 0, p == 15)
+    for s in range(4):
+        act(r("QS", 256 * s, 256 * s + 256), (r("X2", 0, TW), r("XL", 16 * s, 16 * s + 16)))
+    cp(r("uI"), r("pW", 0, 128))
+    ts(r("uA"), r("uI"), 4095, OP.bitwise_and)
+    ts(r("u32"), r("uA"), 32.0, OP.add)
+    ts(r("uM"), r("uA"), -2048.0, OP.add)
+    act(r("SXT"), r("pC", 0, 128), AF.Identity, bias=-2048.0)
+    for s in range(4):
+        tt(r("pr", 16 * s, 16 * s + 16), r("u32", s, 128, 8), r("OC", s, 128, 8), OP.mult)
+    dma("Y", T["AA"][3::16, 1:TW + 1], T["uM"][:], [r("uM")], [r("AA", 1, TW + 1)], "gAA", 64 * KB)
+    for h in range(2):
+        dma("Y", T["SXD"][:, TW * h:TW * h + TW], T["SXT"][:], [r("SXT")], [r("SXD", TW * h, TW * h + TW)], "gSD", 64 * KB)
     for k in range(16):
         d = 613 * k % TW
-        dma("Y", T["SXS"][k::16, :], T["SXF"][k::16, d:d + TW], [r("SXF")], [r("SXS")], "gSX")
-    own_v(0, range(0, W0))
-    for s in range(1, 4):
-        uw_p(s)
+        dma("Y", T["SXS"][k::16, :], T["SXD"][:, d:d + TW], [r("SXD")], [r("SXS")], "gSX", 16 * KB)
+    ts(r("bs"), r("pr"), 5, OP.arith_shift_right, TW - 1, OP.bitwise_and)
+    for k in range(16):
+        ts(r("OL", 64 * k, 64 * k + 64), r("bs"), float(613 * k % TW), OP.add)
+    ready(r("QS", 0, 256), NG)
 
     for t in range(4):
-        if t == 0:
-            u, kn, ow = r("U", 0, 256), r("KN", 0, 256), r("OWB", 0, TW, 8)
-        else:
-            u, kn, ow = r("pE", 0, 256), r("pW", 128, 384), r("ow")
-            a, b = 64 * (t - 1), 64 * t
-            Q["V"].wait_ge(T.sem["arr%d" % (t - 1)], len(topo.engines(T.cores[(rank - t) % N], core)))
-            tt(r("bt"), r("ARR", a, b), r("R", 4 + t - 1, TW, 32), OP.max)
-            ts(r("R", 4 + t - 1, TW, 32), r("bt"), 2047, OP.bitwise_and)
-        cp(r("e"), (r("R", 0, TW), r("AL", 0, 16)))
+        own(t)
+        if t > 0:
+            tt(r("bt"), r("ARR", 64 * (t - 1), 64 * t), r("R", 4 + t - 1, TW, 32), OP.min)
+            ts(r("R", 4 + t - 1, TW, 32), r("bt"), TW - 1, OP.bitwise_and)
+        move(ES, r("e"), (r("R", 0, TW), aL))
         tt(r("prod"), r("e"), u, OP.mult)
-        ts(r("pl"), r("prod"), 5, OP.arith_shift_right, 2047, OP.bitwise_and)
+        ts(r("pl"), r("prod"), 5, OP.arith_shift_right, TW - 1, OP.bitwise_and)
         ts(r("pl16"), r("pl"), r("ck"), OP.add)
-        if t < 3:
-            utab_p(t + 1)
-        Ke = r("pK", 0, 256)
-        mm(Ke, r("CSE"), r("ON"), True, False)
-        mm(Ke, r("I0"), ow, False, False)
-        mm(Ke, r("IZ"), r("e"), False, False)
-        mm(r("pE", 0, 256), r("B0"), r("e"), True, True)
-        lastm = [x for x in PLAN if x[0] == "M"][-1]
-        for x in PLAN:
-            if x[0] == "Vq":
-                lo, hi = x[1:]
-                tt(r("DD", 16 * lo, 16 * hi), (r("X2"), r("pl16", lo, hi)), r("QX", 16 * lo, 16 * hi), OP.subtract)
-            elif x[0] == "Vg":
-                lo, hi = x[1:]
-                cp(r("XG", 16 * lo, 16 * hi), (r("X2"), r("pl16", lo, hi)))
-            elif x[0] == "Sg":
-                lo, hi = x[1:]
-                act(r("XG", 16 * lo, 16 * hi), (r("X2"), r("pl16", lo, hi)))
-            elif x[0] == "Q":
-                lo, hi = x[1:]
-                act(r("AD", 16 * lo, 16 * hi), r("DD", 16 * lo, 16 * hi), AF.Abs)
-            elif x[0] == "D":
-                lo, b, h = x[1], "pD%d" % x[2], x[1] // 128
-                mm(r(b), r("ID"), r("XG", 16 * lo, 16 * lo + 512), True, False)
-                mm(r(b), r("QT", 128 * h, 128 * h + 128), r("E", 16 * (lo - 128 * h), 16 * (lo - 128 * h) + 512), False, True)
-            elif x[0] == "A":
-                act(r("AD", 16 * x[1], 16 * x[1] + 512), r("pD%d" % x[2]), AF.Abs)
-            elif x[0] == "M":
-                lo, hi = x[1:]
-                for k in range(16):
-                    mm(r("pK", lo, hi), Z("Z4", k), r("AD", 16 * lo + k, 16 * hi, 16), False, x is lastm and k == 15)
-            elif t > 0:
-                own_w(t)
-                own_k(t)
-                act(r("kn"), (r("KN", 0, 256 * (t + 1)), r("VT16")))
-                mm(kn, r("IDF"), r("kn"), True, True)
-        if t == 0:
-            ts(r("Z8"), CI, r("c15"), OP.is_equal, 8192.0, OP.mult)
-            op("V", lambda: g.vector.memset(ap(r("F", 256, 264)), -4096), [], [r("F", 256, 264)])
-            ts(r("th4"), r("thI"), 4096.0, OP.mult, -float(1 << 24), OP.add)
-            own_v(0, range(W0, KV))
-            act(r("AA", TW, TW + 256), r("AA", 1, TW, 8))
-            act(r("AB"), (r("AA", 0, TW + 256), r("AL")))
-            wrap()
-            own_sg(0, SA + SB)
-            own_p(0, range(KV), True)
-            own_sd(0, SA + SB)
-            own_sa(SA + SB)
-            own_p(0, SA + SB, False, True)
-        if t < 3:
-            utab_v(t + 1)
-        tt(r("eqs"), r("e"), r("pE", 0, 256), OP.is_equal)
-        if t == 0:
-            own_w(0)
-            lists(1, 4)
-            own_k(0)
-            for s in range(1, 4):
-                qs(s)
-                act(r("AA", TW + 256 * s, TW + 256 * s + 256), r("AA", s + 1, TW, 8))
-            act(r("aB"), (r("IOT"), r("AL", 0, 16)))
-        tt(r("xk"), r("eqs"), kn, OP.mult)
-        cp(r("Aw"), r("pW", 0, 32))
-        tt(r("dA"), r("Aw", 16, 32), r("Aw", 0, 16), OP.subtract)
-        n1 = N1[t]
-        if t < 3:
-            own_v(t + 1, range(0, n1))
-            own_sg(t + 1, SA)
-        tt(r("m"), r("xk"), Ke, OP.min)
-        ts(r("hit"), r("m"), r("th4") if t == 0 else r("thb"), OP.is_lt)
-        mm(r("pC", 0, 256), r("BO"), r("hit"), True, True)
-        cw = r("pE", 256, 272)
+        mm(Ke, r("IZ"), r("e"), True, False)
+        mm(Ke, r("LO"), MV, False, False)
+        mm(pd, r("PD"), r("e"), True, False)
+        mm(pd, r("BO2"), MV, False, True)
+        act(r("pen"), pd, AF.Abs)
+        tt(r("xk"), (r("KN"), vtL), r("pen"), OP.add)
+        mm(c2, r("ID"), r("ci"), True, False)
+        mm(c2, r("ON"), r("c32"), False, False)
+        for n, (lo, hi, who, sub) in enumerate(PLAN):
+            x = (r("X2"), r("pl16", lo, hi))
+            if sub != "P":
+                tt(r("DD", 16 * lo, 16 * hi), x, r("QX", 16 * lo, 16 * hi), OP.subtract)
+                if sub == "V":
+                    act(r("AD", 16 * lo, 16 * hi), r("DD", 16 * lo, 16 * hi), AF.Abs)
+                else:
+                    ts(r("AD", 16 * lo, 16 * hi), r("DD", 16 * lo, 16 * hi), 0.0, OP.max, 2.0, OP.mult)
+                    for k in range(16):
+                        mm(r("pK", lo, hi), Z("ZN", k), r("DD", 16 * lo + k, 16 * hi, 16), False, False)
+                continue
+            move(who, r("XG", 16 * lo, 16 * hi), x)
+            for a in range(lo, hi, 32):
+                b, h, p = r("pD%d" % (a // 32 % 2)), a // 128, a % 128
+                mm(b, r("ID"), r("XG", 16 * a, 16 * a + 512), True, False)
+                mm(b, rp("QT", 128 * h, 128 * h + 128, p, p + 32), rp("E", 0, 512, p, p + 32), False, True)
+                act(r("AD", 16 * a, 16 * a + 512), b, AF.Abs)
+        for lo, hi in SUMS:
+            for k in range(16):
+                mm(r("pK", lo, hi), Z("Z4", k), r("AD", 16 * lo + k, 16 * hi, 16), False, (lo, hi) == SUMS[-1] and k == 15)
+        act(r("AB", 0, 256), (r("AA", 0, TW), aL))
         for p in range(16):
-            mm(cw, Z("Z1", p), r("hit", p, 256, 16), p == 0, p == 15)
-        ts(r("F", 0, 256), r("m"), 2047, OP.bitwise_and)
-        ts(r("fitb"), r("pC", 0, 256), 7.5, OP.is_ge)
-        op("V", lambda: g.vector.tensor_tensor_scan(ap(r("cum")), ap(r("fitb")), ap(r("fitb")), 0.0, OP.add, OP.max),
-           [r("fitb")], [r("cum")])
-        for c in range(4):
-            act(r("junk", 256 * c, 256 * c + 256), r("cum"), AF.Sign, bias=r("jc", c, c + 1), scale=-1.0, acc=r("acc", c, c + 1))
-        ts(r("fit"), cw, 7.5, OP.is_ge)
-        ts(r("nf"), cw, 7.5, OP.is_lt, float(DUMP), OP.mult)
-        if t < 3:
-            ts(r("f256"), cw, 7.5, OP.is_ge, 256.0, OP.mult)
-        tt(r("tA"), r("fit"), r("dA"), OP.mult)
-        tt(r("vsw"), r("vw"), r("nf"), OP.add)
-        if t < 3:
-            tt(r("vtw"), r("vtw"), r("f256"), OP.add)
-        tt(r("aw"), r("tA"), r("Aw", 0, 16), OP.add)
-        tt(r("vw"), r("vw"), r("fit"), OP.add)
-        if t < 3:
-            cp(r("VT16"), r("vtw"))
-            ts(r("AL", 16, 32), r("vtw"), float(TW), OP.add)
-        cp(r("AL", 0, 16), r("aw"))
-        cp(r("VS16"), r("vsw"))
-        if t < 3:
-            own_sd(t + 1, SA)
-            own_sa(SA)
-            own_v(t + 1, range(n1, n1 + W1))
-        else:
-            scatter(r("AA"), r("VS16"), r("aB"))
-        ts(r("inv16", 0, 4), r("acc"), 0.5, OP.mult, 128.0, OP.add)
-        snd = r("SND", 64 * t, 64 * t + 64)
-        ts(snd, (r("F"), r("inv16", 0, 4)), 4096.0, OP.add)
-        dst = T.cores[(rank + 1 + t % (N - 1)) % N]
+            mm(r("pW", 0, 32), Z("ZA", p), r("AB", p, 512, 16), p == 0, p == 15)
+        act(r("Aw"), r("pW", 0, 32))
+        act(r("aB"), (r("IOT"), aL))
+        tt(r("dA"), r("Aw", 16, 32), r("Aw", 0, 16), OP.subtract)
+        tt(r("m"), r("xk"), Ke, OP.min)
+        ts(r("hit"), r("m"), r("th4") if t == 0 else r("thb"), OP.is_lt, -0.125, OP.mult)
+        for p in range(16):
+            mm(c2, Z("Z4", p), r("hit", p, 256, 16), False, p == 15)
+        ts(r("F"), r("m"), TW - 1, OP.bitwise_and)
+        ts(r("fit"), c2, 128.0, OP.is_lt)
+        ts(r("nf"), c2, 128.0, OP.is_ge, float(TW + 1), OP.mult)
+        op("V", lambda: g.vector.tensor_tensor_scan(ap(r("cum")), ap(r("fit")), ap(r("ZR", 0, 16)), -1.0, OP.add, OP.add),
+           [r("fit"), r("ZR", 0, 16)], [r("cum")], 0.07)
+        mm(off, r("LT"), col("cum", 15), True, True)
+        tt(r("top"), r("cum"), c2, OP.max)
+        ts(r("pos"), r("top"), off, OP.add, r("rF"), OP.add)
+        w0 = 64 * (3 - t)
+        scatter(r("SND", w0, w0 + 4352), r("pos"), r("m"))
+        dst, src = T.cores[(rank + 1 + t % (N - 1)) % N], T.cores[(rank - 1 - t % (N - 1)) % N]
         rid, pid = topo.addr(dst, core)
-        last = log["SND"][-1]
-        learn("G", "V", last[4], last[5])
-        g.remote_dma(ap(r("ARR", 64 * t, 64 * t + 64)), ap(snd), T.sem["arr%d" % t], T.sem["snd"], pid, rid, topo.mask(core, dst))
+        op("G", lambda t=t, w0=w0, dst=dst, rid=rid, pid=pid: g.remote_dma(
+            ap(r("ARR", 64 * t, 64 * t + 64)), ap(r("SND", w0, w0 + 64)), T.sem["arr%d" % t], T.sem["snd"], pid, rid, topo.mask(core, dst)),
+           [r("SND", w0, w0 + 64)], [r("ARR", 64 * t, 64 * t + 64)], 0.05, late=FLIGHT,
+           send=(len(topo.engines(core, dst)), ("arr%d" % t, len(topo.engines(src, core)))))
+        tt(v1, v1, r("fit"), OP.add)
+        tt(r("vs"), v1, r("nf"), OP.add)
+        ts(r("VS"), r("vs"), -2.0, OP.add)
+        tt(r("tA"), r("fit"), r("dA"), OP.mult)
+        tt(aw, r("tA"), r("Aw", 0, 16), OP.add)
+        scatter(r("R"), r("VS"), r("F"))
         if t < 3:
-            mm(r("pE", 288, 304), r("ONF", 0, 128), r("fit"), True, True)
-            scatter(r("AA"), r("VS16"), r("aB"))
-            op("V", lambda: g.vector.tensor_reduce(ap(r("bsum")), ap(r("pE", 288, 304)), AxisListType.X, OP.add),
-               [r("pE", 288, 304)], [r("bsum")])
-        scatter(r("R"), r("VS16"), r("F", 0, 256))
-        if t < 3:
-            s, n = t + 1, 256 * (t + 2)
-            act(r("q"), (r("QS", 0, n), r("VT16")))
-            turn(r("q"))
-            act(r("u"), (r("U", 0, n), r("VT16")))
-            mm(r("pE", 0, 256), r("IDF"), r("u"), True, True)
-            if t == 0:
-                for c in range(4):
-                    act(r("OWN", 256 * c, 256 * c + 256), r("OWB", c, TW, 8))
-            act(r("AB"), (r("AA", 0, TW + n), r("AL")))
-            own_p(s, list(range(0, n1 + W1)) + SA, True)
-            spread(r("q"), NG)
-            own_sg(s, SB)
-            own_sd(s, SB)
-            wrap()
-            act(r("ow"), (r("OWN", 0, n), r("VT16")))
-            own_sa(SB)
-            act(r("aB"), (r("IOT"), r("AL", 0, 16)))
-            own_v(s, range(n1 + W1, n1 + W1 + 1))
-            cp(r("bI", 0, 1), r("bsum"))
-            own_v(s, range(n1 + W1 + 1, n1 + W1 + 2))
-            ts(r("bI", 1, 2), r("bI", 0, 1), 255, OP.bitwise_and)
-            own_v(s, range(n1 + W1 + 2, KV))
-            ts(r("thb"), r("bI", 1, 2), 4096.0, OP.mult, r("th4"), OP.add)
-            own_p(s, SB + list(range(n1 + W1, KV)), False, True)
+            mm(tot, r("ON"), col("cum", 15), True, True)
+            ts(col("bI", 0), tot, 128.0, OP.add)
+            ts(col("bI", 1), col("bI", 0), 255, OP.bitwise_and)
+            ts(r("thb"), col("bI", 1), 4096.0, OP.mult, r("th4"), OP.add)
+            tt(vt, vt, r("fit"), OP.add)
+            ts(v0L, v1, -1.0, OP.add)
+            cp(v1L, v1)
+            cp(vtL, vt)
+            cp(aL, aw)
+            act(r("q"), (r("X2", 0, TW), v0L))
+            ready(r("q"), NG)
+        scatter(r("AA"), r("VS"), r("aB"))
 
-    cp(r("VT16"), r("vw"))
+    dma("Y", T["ya"][:], T["W"][:, 0:16], [aw], [], "oL", 8 * KB)
+    ts(r("YV"), v1, -1.0, OP.add)
+    dma("Y", T["yv"][:], T["YV"][:], [r("YV")], [], "oV", 8 * KB)
+    for s in range(2):
+        act(r("pD%d" % s, 0, 256), r("R", 2 + s, TW, 8), AF.Copy, scale=4096.0)
+        tt(r("YR", s, 512, 2), r("pD%d" % s, 0, 256), r("R", s, TW, 8), OP.add)
+    dma("Y", T["yr"][:], T["YR"][:], [r("YR")], [], "oR", 256 * KB)
     for s in range(4):
         act(r("YA", s, 1024, 4), r("AA", s, TW, 8))
-    dma("Y", T["yan"][:], T["YA"][0::16, :], [r("YA")], [], "oA")
-    for s in range(2):
-        ts(r("junk", 256 * s, 256 * s + 256), r("R", 2 + s, TW, 8), 4096.0, OP.mult)
-    for s in range(2):
-        tt(r("YR", s, 512, 2), r("junk", 256 * s, 256 * s + 256), r("R", s, TW, 8), OP.add)
-    dma("Y", T["yr"][:], T["YR"][:], [r("YR")], [], "oR")
-    act(r("YL"), (r("IOT"), r("AL", 0, 16)))
-    act(r("YV"), (r("IOT"), r("VT16")))
-    dma("Y", T["ya"][:], T["YL"][0::16, :], [r("YL")], [], "oL")
-    dma("Y", T["yv"][:], T["YV"][0::16, :], [r("YV")], [], "oV")
+    dma("S", T["yan"][:], T["YA"][0::16, :], [r("YA")], [], "oA", 32 * KB)
     for t in range(3):
-        cp(r("YH", t, 256, 4), r("R", 4 + t, TW, 32))
-    Q["V"].wait_ge(T.sem["arr3"], len(topo.engines(T.cores[(rank - 4) % N], core)))
-    tt(r("bt"), r("ARR", 192, 256), r("R", 7, TW, 32), OP.max)
-    ts(r("R", 7, TW, 32), r("bt"), 2047, OP.bitwise_and)
-    cp(r("YH", 3, 256, 4), r("R", 7, TW, 32))
-    dma("Y", T["yh"][:], T["YH"][:], [r("YH")], [], "oH")
-    for grp in DMAS:
-        g.wait_ge(T.sem[grp], 16 * DMAS[grp])
-    for e in "VSPG":
-        g.wait_ge(T.sem[e], count[e])
-    g.wait_ge(T.sem["snd"], sum(len(topo.engines(core, T.cores[(rank + 1 + t) % N])) for t in range(4)))
+        act(r("YH", t, 256, 4), r("R", 4 + t, TW, 32))
+    tt(r("bt"), r("ARR", 192, 256), r("R", 7, TW, 32), OP.min)
+    ts(r("b3"), r("bt"), TW - 1, OP.bitwise_and)
+    cp(r("YH", 3, 256, 4), r("b3"))
+    dma("Y", T["yh"][:], T["YH"][:], [r("YH")], [], "oH", 128 * KB)
+    issue()

@@ -2,46 +2,54 @@ from concourse.mybir import AluOpType as OP, ActivationFunctionType as AF
 
 TW = 2048
 BIG = float(1 << 25)
-KV = 10
-NG = 10
-XB = "SV"
-ES = "V"
-PLAN = ((128, 160, "S", "P"), (160, 192, "S", "P"), (192, 224, "S", "P"), (224, 256, "V", "P"), (0, 64, "V", "V"), (64, 128, "V", "V"))
-SUMS = ((128, 192), (192, 256), (0, 64), (64, 128))
-CYC, GATHER, SCATTER, PEC, HOP, DFIX, DBW, FLIGHT = 0.00083, 1.5, 3.5, 0.00042, 0.11, 0.9, 350e3, 1.7
+K0 = -255 << 15
+KV = 9
+NQ = 64
+PIECES = (64, 96, 128, 160, 192, 224, 32, 0)
+WHO = ("VSVSVVVV", "VSVSVVqq", "VSVSVVqq", "VSVSVVqq")
+SUMS = ((64, 128), (128, 192), (192, 256), (0, 64))
+TAIL = ((64, 256), (0, 64))
+XB = "DD"
+NBS, PAIR, ES, NM = 2, 2, "VVVV", 4
+OUTS = "VLRHA"
+CYC, GATHER, SCATTER, PEC, HOP, DFIX, DBW, FLIGHT, ROUNDS = 0.00083, 1.4, 3.0, 0.00042, 0.11, 0.9, 350e3, 2.0, 4
 SCRATCH = {}
 for _n, _w, _d in (
     ("X2", 4096, "bfloat16"), ("R", 4096, "int32"), ("AA", 4096, "int32"), ("IOT", 2048, "int32"), ("SXS", 2048, "float32"),
-    ("KN", 1024, "float32"), ("QS", 1024, "bfloat16"), ("MX", 8192, "bfloat16"), ("XS", 4096, "bfloat16"),
-    ("QX", 4096, "bfloat16"), ("XG", 4096, "bfloat16"), ("DD", 4096, "bfloat16"), ("AD", 4096, "bfloat16"),
-    ("SND", 4608, "int32"), ("ARR", 256, "int32"), ("OL", 1024, "uint16"), ("sx", 256, "float16"),
+    ("KN", 1024, "float32"), ("QS", 2048, "bfloat16"), ("MX", 8192, "bfloat16"), ("XS", 4096, "bfloat16"),
+    ("QX", 16 * NQ, "bfloat16"), ("XG", 4096, "bfloat16"), ("DD", 16 * NQ, "bfloat16"), ("AD", 4096, "bfloat16"),
+    ("SND", 4608, "int32"), ("ARR", 256, "int32"), ("OLD", 256, "int32"), ("sx", 256, "float16"),
     ("q", 256, "bfloat16"), ("QT", 256, "bfloat16"), ("AB", 512, "float16"), ("aB", 256, "float32"), ("e", 256, "float16"),
     ("prod", 256, "int32"), ("pl", 256, "int32"), ("pl16", 256, "uint16"), ("pen", 256, "float32"), ("xk", 256, "float32"),
     ("m", 256, "int32"), ("hit", 256, "bfloat16"), ("F", 256, "int32"),
     ("fit", 16, "float32"), ("cum", 16, "bfloat16"), ("top", 16, "float32"), ("pos", 16, "uint16"), ("nf", 16, "float32"),
     ("vs", 16, "float32"), ("VS", 16, "uint16"), ("Aw", 32, "float32"), ("dA", 16, "float32"), ("tA", 16, "float32"),
     ("W", 48, "float32"), ("AL", 64, "uint16"), ("bI", 2, "int32"), ("th4", 1, "float32"), ("thb", 1, "float32"),
-    ("bt", 64, "int32"), ("b3", 64, "int32"), ("thI", 1, "int32"), ("wI", 1, "int32"), ("wF", 1, "float32"),
+    ("thI", 1, "int32"), ("wI", 1, "int32"), ("wF", 1, "float32"),
     ("pI", 1, "int32"), ("pF", 1, "float32"), ("rI", 1, "int32"), ("rF", 1, "float32"), ("q16", 1, "float32"),
-    ("nr0", 1, "float32"), ("lu", 1, "float32"), ("kI", 2, "int32"), ("ck", 1, "float32"), ("OH", 16, "float32"),
-    ("CI", 144, "float32"), ("CB", 128, "float32"), ("C16", 16, "float32"), ("XI", 128, "int32"), ("XL", 64, "uint16"),
-    ("ci", 16, "bfloat16"), ("c32", 16, "bfloat16"), ("r32", 2, "int32"), ("p32", 1, "float32"), ("EI", 512, "bfloat16"),
+    ("nr0", 1, "float32"), ("lu", 1, "float32"), ("nb", 1, "float32"), ("kI", 2, "int32"), ("ck", 1, "float32"),
+    ("OH", 16, "float32"), ("CI", 144, "float32"), ("CB", 128, "float32"), ("C16", 16, "float32"), ("XI", 128, "int32"),
+    ("XL", 64, "uint16"), ("ci", 16, "bfloat16"), ("r32", 1, "int32"), ("p32", 1, "float32"), ("EI", 512, "bfloat16"),
     ("E", 512, "bfloat16"), ("Z1", 144, "bfloat16"), ("Z4", 144, "bfloat16"), ("ZW", 144, "bfloat16"), ("ZA", 144, "bfloat16"),
-    ("BO", 128, "bfloat16"), ("BO2", 128, "bfloat16"), ("BQ", 128, "bfloat16"), ("LU", 128, "bfloat16"), ("LO", 128, "bfloat16"),
-    ("PD", 128, "bfloat16"), ("LT", 128, "bfloat16"), ("ID", 128, "bfloat16"), ("NI", 128, "bfloat16"), ("IZ", 128, "bfloat16"),
-    ("ON", 128, "bfloat16"), ("ZR", 128, "bfloat16"), ("N2", 128, "bfloat16"), ("ZN", 144, "bfloat16"),
+    ("ZC", 144, "bfloat16"), ("BO", 128, "bfloat16"), ("BO2", 128, "bfloat16"), ("BN", 128, "bfloat16"), ("BP", 128, "bfloat16"),
+    ("LU", 128, "bfloat16"), ("LO", 128, "bfloat16"), ("PD", 128, "bfloat16"), ("PB", 128, "bfloat16"), ("LT", 128, "bfloat16"),
+    ("ID", 128, "bfloat16"), ("NI", 128, "bfloat16"), ("IZ", 128, "bfloat16"), ("N2", 128, "bfloat16"),
+    ("ON", 128, "bfloat16"), ("ZR", 128, "bfloat16"),
     ("AC", 128, "int32"), ("OC", 128, "int32"), ("uI", 128, "int32"), ("uA", 128, "int32"), ("uM", 128, "int32"),
-    ("u32", 128, "float32"), ("pr", 64, "int32"), ("bs", 64, "int32"), ("SXT", 128, "float32"),
-    ("YR", 512, "float32"), ("YH", 256, "float32"), ("YA", 1024, "float32"), ("YV", 16, "float32"),
+    ("u32", 128, "float32"), ("SXT", 128, "float32"),
+    ("YR", 512, "float32"), ("YH", 256, "float32"), ("YA", 3088, "float32"), ("YV", 16, "float32"),
+    ("y0", 16, "float32"), ("y4", 16, "float32"), ("YL", 16, "uint16"),
 ):
     SCRATCH[_n] = ("sbuf", [128, _w], _d)
+SCRATCH["OL"] = ("sbuf", [128, 4, 256], "uint16")
+SCRATCH["pr"] = SCRATCH["bs"] = ("sbuf", [128, 4, 16], "int32")
 SCRATCH["SXD"] = ("dram", [8, 2 * TW], "float32")
 PSUM = ("pK", "pE", "pO", "pD0", "pD1", "pD2", "pC", "pW")
 for _n in PSUM:
     SCRATCH[_n] = ("psum", [128, 512], "float32")
-DMAS = {"lAC": 1, "lOC": 1, "lW": 1, "lT": 1, "lX": 1, "lXb": 1, "lR": 1, "gAA": 3, "gSD": 2, "gSX": 16,
+DMAS = {"lAC": 1, "lOC": 1, "lW": 1, "lT": 1, "lX0": 1, "lX1": 1, "lB0": 1, "lB1": 1, "lR": 1, "gAA": 3, "gSD": 2, "gSX": 16,
         "oR": 1, "oH": 1, "oA": 1, "oV": 1, "oL": 1}
-SEMAPHORES = ["V", "S", "P", "G", "snd"] + ["arr%d" % t for t in range(4)] + list(DMAS)
+SEMAPHORES = ["V", "S", "P", "G", "snd"] + [x + str(t) for x in ("arr", "pre") for t in range(4)] + list(DMAS)
 _ORDER = []
 
 
@@ -73,26 +81,39 @@ def _place(busy, t, d):
 
 
 def _order(calls):
-    way = [0.0] * len(calls)
-    for i in range(len(calls) - 1, -1, -1):
+    every, best = range(len(calls)), None
+    way = [0.0 for _ in every]
+    for i in reversed(every):
         c = calls[i]
         way[i] += c["cost"] + c["late"]
         for j in c["wait"]:
             way[j] = max(way[j], way[i] + HOP)
         for j in c["after"]:
             way[j] = max(way[j], way[i] - calls[j]["late"])
-    busy = {k: [] for k in "VSPGYD"}
-    start, free, done = {}, {}, {}
-    for i in sorted(range(len(calls)), key=lambda i: (-way[i], i)):
-        c = calls[i]
-        t = max([0.0] + [done[j] + HOP for j in c["wait"]] + [free[j] for j in c["after"]])
-        start[i] = _place(busy[c["eng"]], t, c["cost"])
-        free[i] = done[i] = start[i] + c["cost"]
-        if c["ring"]:
-            done[i] = _place(busy["D"], free[i] + DFIX / 2, c["ring"]) + c["ring"] + DFIX / 2
-        elif c["late"]:
-            done[i] += c["late"]
-    return sorted(range(len(calls)), key=lambda i: (start[i], i))
+    for _ in range(ROUNDS):
+        busy = {k: [] for k in "VSPGY"}
+        start, free, done, rings = {}, {}, {}, 0.0
+        for i in sorted(every, key=lambda i: (-way[i], i)):
+            c = calls[i]
+            t = max([0.0] + [done[j] + HOP for j in c["wait"]] + [free[j] for j in c["after"]])
+            start[i] = _place(busy[c["eng"]], t, c["cost"])
+            free[i] = start[i] + c["cost"]
+            done[i] = free[i] + c["late"]
+            if c["ring"]:
+                rings = max(rings, free[i] + DFIX / 2) + c["ring"]
+                done[i] = rings + DFIX / 2
+        if best is None or max(done.values()) < best[0]:
+            best = (max(done.values()), sorted(every, key=lambda i: (start[i], i)))
+        busy = {k: [] for k in "VSPGY"}
+        back = [calls[i]["late"] for i in every]
+        for i in sorted(every, key=lambda i: (-free[i], -i)):
+            c = calls[i]
+            way[i] = _place(busy[c["eng"]], back[i], c["cost"]) + c["cost"]
+            for j in c["wait"]:
+                back[j] = max(back[j], way[i] + HOP + done[j] - free[j])
+            for j in c["after"]:
+                back[j] = max(back[j], way[i])
+    return best[1]
 
 
 def rank_program(g, core, T, topo):
@@ -115,6 +136,9 @@ def rank_program(g, core, T, topo):
         if len(x) == 6:
             return T[x[0]][x[4]:x[5], x[1]:x[2]]
         n, lo, hi, st = x
+        if len(SCRATCH[n][1]) == 3:
+            w = SCRATCH[n][1][2]
+            return T[n][:, lo // w, lo % w:lo % w + hi - lo]
         return T[n][:, lo:hi:st] if st > 1 else T[n][:, lo:hi]
 
     def flat(xs):
@@ -148,10 +172,10 @@ def rank_program(g, core, T, topo):
                 elif (bank and c["eng"] != eng) or ((wr or w2) and _meet(acc[1:], sp)):
                     for k in groups.get(c["grp"], [j]):
                         wait[k] = acc[0]
-        if ring or send is not None:
-            if eng in lastdma:
-                after.add(lastdma[eng])
-            lastdma[eng] = me
+        if ring or send:
+            if bool(ring) in lastdma:
+                after.add(lastdma[bool(ring)])
+            lastdma[bool(ring)] = me
         if grp is not None:
             groups.setdefault(grp, []).append(me)
         calls.append(dict(eng=eng, fn=fn, cost=cost, late=late + (ring and ring + DFIX), ring=ring, grp=grp, send=send, wait=wait, after=after))
@@ -172,17 +196,17 @@ def rank_program(g, core, T, topo):
         for i in _ORDER:
             c = calls[i]
             kn = known[c["eng"]]
-            need = [mark[j]["ARR" if calls[j]["send"] is not None and name == "ARR" else ""] for j, name in c["wait"].items()]
+            need = [mark[j].get(name, mark[j][""]) for j, name in c["wait"].items()]
             for sem, val, clock in sorted(need, key=lambda x: (-len(x[2]), -x[1])):
                 if kn.get(sem, 0) < val:
                     Q[c["eng"]].wait_ge(T.sem[sem], val)
                     for s, x in list(clock.items()) + [(sem, val)]:
                         kn[s] = max(kn.get(s, 0), x)
             ins = c["fn"]()
-            if c["send"] is not None:
-                out, inn = c["send"]
+            if c["send"]:
+                out, tile, sem, inn = c["send"]
                 sent += out
-                mark[i] = {"": ("snd", sent, dict(kn)), "ARR": (inn[0], inn[1], {})}
+                mark[i] = {"": ("snd", sent, dict(kn)), tile: (sem, inn, {})}
             elif c["grp"] is not None:
                 ins.then_inc(T.sem[c["grp"]], 16)
                 mark[i] = {"": (c["grp"], 16 * DMAS[c["grp"]], dict(kn))}
@@ -199,22 +223,22 @@ def rank_program(g, core, T, topo):
     def sc(x):
         return ap(x) if isinstance(x, tuple) else x
 
-    def vcost(o, a, per):
+    def vcost(a, per):
         if len(a) == 2:
             return 0.05 + CYC * GATHER * width(a)
         return 0.02 + CYC * max(64, per * width(a))
 
     def tt(o, a, b, f):
         per = 1 if a[0] in PSUM or b[0] in PSUM else 2
-        op("V", lambda: g.vector.tensor_tensor(out=ap(o), in0=ap(a), in1=ap(b), op=f), [a, b], [o], vcost(o, a, per))
+        op("V", lambda: g.vector.tensor_tensor(out=ap(o), in0=ap(a), in1=ap(b), op=f), [a, b], [o], vcost(a, per))
 
     def ts(o, a, s1, f, s2=None, f2=None):
         kw = {} if f2 is None else {"op1": f2}
         op("V", lambda: g.vector.tensor_scalar(out=ap(o), in0=ap(a), scalar1=sc(s1), scalar2=sc(s2), op0=f, **kw), [a, s1, s2], [o],
-           vcost(o, a, 0.5 if short(o, a) else 1))
+           vcost(a, 0.5 if short(o, a) else 1))
 
     def cp(o, a):
-        op("V", lambda: g.vector.tensor_copy(out=ap(o), in_=ap(a)), [a], [o], vcost(o, a, 0.5 if len(a) > 2 and short(o, a) else 1))
+        op("V", lambda: g.vector.tensor_copy(out=ap(o), in_=ap(a)), [a], [o], vcost(a, 0.5 if len(a) > 2 and short(o, a) else 1))
 
     def scatter(win, off, a):
         op("V", lambda: g.vector.tensor_copy(out=ap((win, off)), in_=ap(a)), [a, off], [win], 0.05 + CYC * SCATTER * width(a))
@@ -238,14 +262,20 @@ def rank_program(g, core, T, topo):
     def dma(eng, out, in_, reads, writes, grp, size):
         op(eng, lambda: Q[eng].dma_start(out=out, in_=in_), reads, writes, 0.05, grp, ring=0.13 + size / DBW)
 
+    def send(o, a, sem, step, late):
+        dst, src = T.cores[(rank + step) % N], T.cores[(rank - step) % N]
+        rid, pid = topo.addr(dst, core)
+        op("G", lambda: g.remote_dma(ap(o), ap(a), T.sem[sem], T.sem["snd"], pid, rid, topo.mask(core, dst)), [a], [o], 0.05,
+           late=late, send=(len(topo.engines(core, dst)), o[0], sem, len(topo.engines(src, core))))
+
     def iota(o, pattern, cm, base=0):
         op("G", lambda: g.iota(ap(o), pattern, base, cm, allow_small_or_imprecise_dtypes=True), [], [o], 0.13 + 2 * CYC * width(o))
 
-    def fill(o, c):
-        iota(o, [[0, o[2] - o[1]]], 0, c)
-
     def sel(o, a, pattern, cmp, base, cm, other=0.0):
         op("G", lambda: g.affine_select(ap(o), ap(a), pattern, cmp, other, base, cm), [a], [o], 0.17 + 2 * CYC * width(o))
+
+    def gcp(o, a):
+        sel(o, a, [[0, width(o)]], OP.is_equal, 0, 0)
 
     def Z(name, k):
         return r(name, 15 - k, 143 - k)
@@ -258,23 +288,28 @@ def rank_program(g, core, T, topo):
     MV = r("AB", 256, 512)
     u, pd = r("pE", 0, 256), r("pE", 256, 512)
     c2, off, tot = r("pC", 0, 16), col("pE", 256), col("pE", 257)
-    Ke = r("pK", 0, 256)
     KB = 1024
 
     dma("S", T["wI"][:], T["w"][:], [], [r("wI")], "lW", 512)
-    dma("S", T["X2"][:, 0:TW], T["xc"][:], [], [r("X2", 0, TW)], "lX", 512 * KB)
+    for h in range(2):
+        dma("YS"[h], T["X2"][:, KB * h:KB * h + KB], T["xc"][:, KB * h:KB * h + KB], [], [r("X2", KB * h, KB * h + KB)], "lX%d" % h, 256 * KB)
     dma("Y", T["OC"][:], T["rf"][0::16, :], [], [r("OC")], "lOC", 64 * KB)
-    dma("Y", T["AC"][:], T["an"][:], [], [r("AC")], "lAC", 64 * KB)
-    if XB == "D":
-        dma("S", T["X2"][:, TW:2 * TW], T["xc"][:], [], [r("X2", TW, 2 * TW)], "lXb", 512 * KB)
-        dma("Y", T["thI"][:], T["th"][:], [], [r("thI")], "lT", 512)
-    else:
-        dma("S", T["thI"][:], T["th"][:], [], [r("thI")], "lT", 512)
-        for h in range(2):
-            move(XB[h], r("X2", TW + 1024 * h, TW + 1024 * h + 1024), r("X2", 1024 * h, 1024 * h + 1024))
+    dma("S", T["AC"][:], T["an"][:], [], [r("AC")], "lAC", 64 * KB)
+    for h in range(2):
+        one, two = r("X2", KB * h, KB * h + KB), r("X2", TW + KB * h, TW + KB * h + KB)
+        if XB[h] == "D":
+            dma("Y", ap(two), T["xc"][:, KB * h:KB * h + KB], [], [two], "lB%d" % h, 256 * KB)
+        else:
+            move(XB[h], two, one)
     dma("Y", T["R"][:, 0:TW], T["rf"][:], [], [r("R", 0, TW)], "lR", KB * KB)
+    dma("Y", T["thI"][:], T["th"][:], [], [r("thI")], "lT", 512)
 
-    op("V", lambda: g.vector.memset(ap(r("AA", 0, TW)), 1), [], [r("AA", 0, TW)], CYC * TW)
+    for h in range(4):
+        x = r("AA", 512 * h, 512 * h + 512)
+        if h < NM:
+            op("V", lambda x=x: g.vector.memset(ap(x), 1), [], [x], CYC * 512)
+        else:
+            iota(x, [[0, 512]], 0, 1)
     iota(r("pI"), [[1, 1]], 1)
     iota(r("pF"), [[1, 1]], 1)
     iota(r("CI"), [[1, 144]], 0)
@@ -282,25 +317,27 @@ def rank_program(g, core, T, topo):
     iota(r("CB"), [[16, 8], [0, 16]], 0)
     iota(r("C16"), [[16, 16]], 0)
     iota(r("EI"), [[1, 32], [0, 16]], 0)
-    C128 = r("CI", 0, 128)
+    iota(r("ZR"), [[0, 128]], 0)
+    iota(r("ON"), [[0, 128]], 0, 1)
+    for h in range(4):
+        iota(r("IOT", 512 * h, 512 * h + 512), [[1, 512]], 0, 512 * h)
     ts(r("rI"), r("pI"), 15, OP.bitwise_and)
     ts(r("XI", 64, 128), r("XI", 0, 64), TW - 1, OP.bitwise_and)
     cp(r("rF"), r("rI"))
     cp(r("XL"), r("XI", 64, 128))
     tt(r("q16"), r("pF"), r("rF"), OP.subtract)
     act(r("wF"), r("wI"))
-    ts(col("r32", 0), r("pI"), 31, OP.bitwise_and)
+    ts(r("r32"), r("pI"), 31, OP.bitwise_and)
     ts(r("Z1"), r("CI"), -15.0, OP.add, r("q16"), OP.is_equal)
     ts(r("OH"), r("CI", 0, 16), r("rF"), OP.is_equal)
-    act(r("ZW"), r("Z1"), AF.Copy, scale=r("wF"))
-    act(r("Z4"), r("Z1"), AF.Copy, scale=4096.0)
-    ts(r("ID"), C128, r("pF"), OP.is_equal)
+    ts(r("ID"), r("CI", 0, 128), r("pF"), OP.is_equal)
     ts(r("BO"), r("CB"), r("q16"), OP.is_equal)
-    cp(r("p32"), col("r32", 0))
+    cp(r("p32"), r("r32"))
     ts(v1, r("XI", 64, 80), 1.0, OP.add)
     ts(vt, r("C16"), r("rF"), OP.add, 4.0, OP.mult)
     ts(r("lu"), col("OH", 4), 2080.0, OP.mult, col("OH", 3), OP.add)
     ts(r("nr0"), r("rF"), 0.0, OP.not_equal)
+    ts(r("nb"), col("OH", 0), -BIG, OP.mult)
     cp(r("AL", 16, 48), r("W", 16, 48))
     cp(aL, r("AC", 0, 128, 8))
     ts(col("kI", 0), r("rI"), 613.0, OP.mult)
@@ -308,76 +345,59 @@ def rank_program(g, core, T, topo):
     cp(r("ck"), col("kI", 1))
     ts(r("E"), r("EI"), r("p32"), OP.is_equal, -1.0, OP.mult)
     ts(r("ci"), r("XI", 64, 80), 0.125, OP.mult, -256.0, OP.add)
-    ts(r("th4"), r("thI"), 4096.0, OP.mult, -float(1 << 24), OP.add)
-    if any(x[3] == "R" for x in PLAN):
-        act(r("ZN"), r("Z1"), AF.Copy, scale=-4096.0)
-    act(r("NI"), r("ID"), AF.Copy, scale=-1.0)
-    act(r("N2"), r("ID"), AF.Copy, scale=-2048.0)
-    act(r("LU"), r("BO"), AF.Copy, scale=r("lu"))
-    act(r("BO2"), r("BO"), AF.Copy, scale=col("OH", 2))
-    act(r("IZ"), r("ID"), AF.Copy, scale=r("nr0"))
-    act(r("ZA"), r("Z1"), AF.Copy, scale=col("OH", 0))
+    ts(r("th4"), r("thI"), 4096.0, OP.mult, K0 - 0.5, OP.add)
+    for o, a, x in (("ZW", "Z1", r("wF")), ("Z4", "Z1", 4096.0), ("ZC", "Z1", -256.0), ("ZA", "Z1", col("OH", 0)),
+                    ("NI", "ID", -1.0), ("N2", "ID", -2048.0), ("IZ", "ID", r("nr0")), ("PD", "ID", BIG),
+                    ("LU", "BO", r("lu")), ("BO2", "BO", col("OH", 2)), ("PB", "BO", r("nb")), ("BN", "BO", -2048.0), ("BP", "BO", 4096.0)):
+        act(r(o), r(a), AF.Copy, scale=x)
+    tt(r("PD"), r("PD"), r("PB"), OP.add)
+    sel(r("BP"), r("BP"), [[0, 8], [1, 16]], OP.is_ge, -KV, 0)
+    sel(r("LO"), r("ZR"), [[-16, 8], [-1000, 16]], OP.not_equal, -2, 1, 1.0)
+    sel(r("LO"), r("LO"), [[-16, 8], [0, 16]], OP.not_equal, -4, 1, float(K0))
+    sel(r("LT"), r("BO"), [[1, 128]], OP.is_gt, 0, -1)
+    act(r("KN"), r("X2", 0, KB), AF.Copy, scale=0.0)
     dma("Y", T["AA"][0::16, 0:TW], T["an"][:], [], [r("AA", 0, TW)], "gAA", 64 * KB)
     dma("Y", T["AA"][2::16, 1:TW + 1], T["rf"][0::16, :], [], [r("AA", 1, TW + 1)], "gAA", 64 * KB)
-    fill(r("ZR"), 0)
-    fill(r("BQ"), -2048)
-    sel(r("BQ"), r("BQ"), [[0, 8], [-1, 16]], OP.is_ge, KV - 1, 0, 2048.0)
-    sel(r("BQ"), r("BQ"), [[-16, 8], [0, 16]], OP.is_ge, 0, 1)
-    sel(r("BQ"), r("BQ"), [[16, 8], [0, 16]], OP.is_ge, 15, -1)
-    sel(r("PD"), r("ZR"), [[-1, 128]], OP.not_equal, 0, 1, BIG)
-    sel(r("PD"), r("PD"), [[-16, 8], [0, 16]], OP.not_equal, 0, 1, -BIG)
-    sel(r("PD"), r("PD"), [[0, 8], [1, 16]], OP.not_equal, 0, 0)
-    sel(r("LO"), r("ZR"), [[-16, 8], [-1000, 16]], OP.not_equal, -2, 1, 1.0)
-    sel(r("LO"), r("LO"), [[-16, 8], [0, 16]], OP.not_equal, -4, 1, -float(1 << 24))
-    fill(r("ON"), 1)
-    fill(r("c32"), 32)
-    sel(r("LT"), r("BO"), [[1, 128]], OP.is_gt, 0, -1)
-    for h in range(4):
-        iota(r("IOT", 512 * h, 512 * h + 512), [[1, 512]], 0, 512 * h)
-    for h in range(2):
-        fill(r("KN", 512 * h, 512 * h + 512), 0)
-    fill(r("SND", 0, 256), 4096)
+    for t in range(4):
+        old = r("OLD", 64 * t, 64 * t + 64)
+        gcp(old, r("R", 4 + t, TW, 32))
+        send(r("SND", 192 - 64 * t, 256 - 64 * t), old, "pre%d" % t, -1 - t % (N - 1), 3 * FLIGHT + 13 * t)
 
-    def ol(s, k):
-        return r("OL", 64 * k + 16 * s, 64 * k + 16 * s + 16)
+    def ol(s, k, n=1):
+        return r("OL", 256 * s + 16 * k, 256 * s + 16 * (k + n))
 
     def own(s):
-        qs, o, m0 = r("QS", 256 * s, 256 * s + 256), r("pO", 0, 256), 4096 * (s % 2)
-        mm(o, r("BQ"), qs, True, False)
+        o, m0 = r("pO", 0, 256), 4096 * (s % 2)
+        mm(o, r("BN"), r("QS", 512 * s, 512 * s + 256), True, False)
+        mm(o, r("BP"), r("QS", 512 * s, 512 * s + 256), False, False)
         act(r("sx"), (r("SXS"), ol(s, 0)))
-        ks = [(k, 1) for k in range(KV)]
+        ks = [(k, min(PAIR, KV - k)) for k in range(0, KV, PAIR)]
         for n, k in enumerate(range(KV, 16, 2)):
-            ks.insert(min(len(ks), 2 * n + 1), (k, 2))
+            ks.insert((4 - PAIR) * n + 1, (k, min(2, 16 - k)))
         for k, n in ks:
-            mx = r("MX", m0 + 256 * k, m0 + 256 * (k + n))
-            if n == 1:
-                tt(mx, (r("X2"), ol(s, k)), qs, OP.max)
+            mx, qs = r("MX", m0 + 256 * k, m0 + 256 * (k + n)), r("QS", 512 * s, 512 * s + 256 * n)
+            if k < KV:
+                tt(mx, (r("X2"), ol(s, k, n)), qs, OP.max)
             else:
-                for h in range(2):
-                    act(r("XS", 256 * (k + h), 256 * (k + h + 1)), (r("X2"), ol(s, k + h)))
-                mm(r("pD2"), r("ID"), r("XS", 256 * k, 256 * k + 512), True, False)
-                for h in range(2):
-                    mm(r("pD2", 256 * h, 256 * h + 256), r("NI"), qs, False, h == 1)
-                act(mx, r("pD2"), AF.Relu)
+                xs, b = r("XS", 256 * k, 256 * (k + n)), r("pD%d" % (2 - (k - KV) // 2 % NBS), 0, 256 * n)
+                act(xs, (r("X2"), ol(s, k, n)))
+                mm(b, r("ID"), xs, True, False)
+                mm(b, r("NI"), qs, False, True)
+                act(mx, b, AF.Relu)
             for h in range(n):
                 mm(o, Z("Z4", k + h), r("MX", m0 + 256 * (k + h), m0 + 256 * (k + h + 1)), False, False)
         mm(o, r("N2"), r("sx"), False, True)
-        act(r("KN", s, 1024, 4), o, AF.Identity, bias=float(2048 - 3 * (1 << 23)), scale=2.0)
+        act(r("KN", s, 1024, 4), o, AF.Identity, bias=float(2048 - (1 << 23) + K0), scale=2.0)
 
-    HALVES = sorted({x[0] // 128 for x in PLAN if x[3] == "P"})
-    NQ = sum(x[1] - x[0] for x in PLAN if x[3] != "P")
+    def key(lo, hi):
+        return r("pK", lo, hi) if TAIL[0][0] <= lo < TAIL[0][1] else r("pC", 256 + lo, 256 + hi)
 
-    def ready(q, ng):
-        for h in HALVES:
-            mm(r("pW", 128 + 128 * h, 256 + 128 * h), (q[0], q[1] + 128 * h, q[1] + 128 * h + 128, 1), r("ID"), True, True)
-        a, b = 128 * HALVES[0], 128 * HALVES[-1] + 128
-        act(r("QT", a, b), r("pW", 128 + a, 128 + b))
-        src = (q[0], q[1], q[1] + NQ, 1)
-        for k in range(16 if NQ else 0):
-            if k < 16 - ng:
-                act(r("QX", k, 16 * NQ, 16), src)
-            else:
-                sel(r("QX", k, 16 * NQ, 16), src, [[0, NQ]], OP.is_equal, 0, 0)
+    def ready(q, t):
+        for h in range(2):
+            mm(r("pW", 128 + 128 * h, 256 + 128 * h), r(q, 128 * h, 128 * h + 128), r("ID"), True, True)
+        act(r("QT"), r("pW", 128, 384))
+        for k in range(16 if "q" in WHO[t] else 0):
+            gcp(r("QX", k, 16 * NQ, 16), r(q, 0, NQ))
         act(MV, (r("AA", 0, TW), v1L))
         mm(u, r("LU"), MV, True, True)
 
@@ -386,7 +406,9 @@ def rank_program(g, core, T, topo):
     for p in range(16):
         mm(r("pC", 0, 128), Z("Z1", p), r("X2", 128 * p, 128 * p + 128), p == 0, p == 15)
     for s in range(4):
-        act(r("QS", 256 * s, 256 * s + 256), (r("X2", 0, TW), r("XL", 16 * s, 16 * s + 16)))
+        one, two = r("QS", 512 * s, 512 * s + 256), r("QS", 512 * s + 256, 512 * s + 512)
+        act(one, (r("X2", 0, TW), r("XL", 16 * s, 16 * s + 16)))
+        (gcp if s else cp)(two, one)
     cp(r("uI"), r("pW", 0, 128))
     ts(r("uA"), r("uI"), 4095, OP.bitwise_and)
     ts(r("u32"), r("uA"), 32.0, OP.add)
@@ -399,59 +421,56 @@ def rank_program(g, core, T, topo):
         dma("Y", T["SXD"][:, TW * h:TW * h + TW], T["SXT"][:], [r("SXT")], [r("SXD", TW * h, TW * h + TW)], "gSD", 64 * KB)
     for k in range(16):
         d = 613 * k % TW
-        dma("Y", T["SXS"][k::16, :], T["SXD"][:, d:d + TW], [r("SXD")], [r("SXS")], "gSX", 16 * KB)
-    ts(r("bs"), r("pr"), 5, OP.arith_shift_right, TW - 1, OP.bitwise_and)
+        dma("Y", T["SXS"][k::16, :], T["SXD"][:, d:d + TW], [r("SXD")], [r("SXS")], "gSX", 64 * KB)
+    op("V", lambda: g.vector.tensor_scalar(out=T["bs"][:], in0=T["pr"][:], scalar1=5, scalar2=TW - 1, op0=OP.arith_shift_right,
+                                           op1=OP.bitwise_and), [r("pr", 0, 64)], [r("bs", 0, 64)], 0.07)
     for k in range(16):
-        ts(r("OL", 64 * k, 64 * k + 64), r("bs"), float(613 * k % TW), OP.add)
-    ready(r("QS", 0, 256), NG)
+        op("V", lambda k=k: g.vector.tensor_scalar(out=T["OL"][:, :, 16 * k:16 * k + 16], in0=T["bs"][:], scalar1=float(613 * k % TW),
+                                                   scalar2=None, op0=OP.add), [r("bs", 0, 64)], [ol(s, k) for s in range(4)], 0.07)
+    ready("QS", 0)
 
     for t in range(4):
         own(t)
         if t > 0:
-            tt(r("bt"), r("ARR", 64 * (t - 1), 64 * t), r("R", 4 + t - 1, TW, 32), OP.min)
-            ts(r("R", 4 + t - 1, TW, 32), r("bt"), TW - 1, OP.bitwise_and)
-        move(ES, r("e"), (r("R", 0, TW), aL))
+            cp(r("R", 4 + t - 1, TW, 32), r("ARR", 64 * t - 64, 64 * t))
+        move(ES[t], r("e"), (r("R", 0, TW), aL))
         tt(r("prod"), r("e"), u, OP.mult)
         ts(r("pl"), r("prod"), 5, OP.arith_shift_right, TW - 1, OP.bitwise_and)
         ts(r("pl16"), r("pl"), r("ck"), OP.add)
-        mm(Ke, r("IZ"), r("e"), True, False)
-        mm(Ke, r("LO"), MV, False, False)
+        for lo, hi in TAIL:
+            mm(key(lo, hi), r("IZ"), r("e", lo, hi), True, False)
+            mm(key(lo, hi), r("LO"), r("AB", 256 + lo, 256 + hi), False, False)
         mm(pd, r("PD"), r("e"), True, False)
         mm(pd, r("BO2"), MV, False, True)
         act(r("pen"), pd, AF.Abs)
         tt(r("xk"), (r("KN"), vtL), r("pen"), OP.add)
-        mm(c2, r("ID"), r("ci"), True, False)
-        mm(c2, r("ON"), r("c32"), False, False)
-        for n, (lo, hi, who, sub) in enumerate(PLAN):
-            x = (r("X2"), r("pl16", lo, hi))
-            if sub != "P":
-                tt(r("DD", 16 * lo, 16 * hi), x, r("QX", 16 * lo, 16 * hi), OP.subtract)
-                if sub == "V":
-                    act(r("AD", 16 * lo, 16 * hi), r("DD", 16 * lo, 16 * hi), AF.Abs)
-                else:
-                    ts(r("AD", 16 * lo, 16 * hi), r("DD", 16 * lo, 16 * hi), 0.0, OP.max, 2.0, OP.mult)
-                    for k in range(16):
-                        mm(r("pK", lo, hi), Z("ZN", k), r("DD", 16 * lo + k, 16 * hi, 16), False, False)
-                continue
-            move(who, r("XG", 16 * lo, 16 * hi), x)
-            for a in range(lo, hi, 32):
-                b, h, p = r("pD%d" % (a // 32 % 2)), a // 128, a % 128
-                mm(b, r("ID"), r("XG", 16 * a, 16 * a + 512), True, False)
+        for a, who in zip(PIECES, WHO[t]):
+            x, lo, hi = (r("X2"), r("pl16", a, a + 32)), 16 * a, 16 * a + 512
+            if who == "q":
+                tt(r("DD", lo, hi), x, r("QX", lo, hi), OP.subtract)
+                act(r("AD", lo, hi), r("DD", lo, hi), AF.Abs)
+            else:
+                b, h, p = r("pD%d" % (a // 32 % 3)), a // 128, a % 128
+                move(who, r("XG", lo, hi), x)
+                mm(b, r("ID"), r("XG", lo, hi), True, False)
                 mm(b, rp("QT", 128 * h, 128 * h + 128, p, p + 32), rp("E", 0, 512, p, p + 32), False, True)
-                act(r("AD", 16 * a, 16 * a + 512), b, AF.Abs)
-        for lo, hi in SUMS:
+                act(r("AD", lo, hi), b, AF.Abs)
+        for n, (lo, hi) in enumerate(SUMS):
+            last = all(key(*x)[0] != key(lo, hi)[0] for x in SUMS[n + 1:])
             for k in range(16):
-                mm(r("pK", lo, hi), Z("Z4", k), r("AD", 16 * lo + k, 16 * hi, 16), False, (lo, hi) == SUMS[-1] and k == 15)
+                mm(key(lo, hi), Z("Z4", k), r("AD", 16 * lo + k, 16 * hi, 16), False, last and k == 15)
         act(r("AB", 0, 256), (r("AA", 0, TW), aL))
         for p in range(16):
             mm(r("pW", 0, 32), Z("ZA", p), r("AB", p, 512, 16), p == 0, p == 15)
         act(r("Aw"), r("pW", 0, 32))
         act(r("aB"), (r("IOT"), aL))
         tt(r("dA"), r("Aw", 16, 32), r("Aw", 0, 16), OP.subtract)
-        tt(r("m"), r("xk"), Ke, OP.min)
-        ts(r("hit"), r("m"), r("th4") if t == 0 else r("thb"), OP.is_lt, -0.125, OP.mult)
+        for lo, hi in TAIL:
+            tt(r("m", lo, hi), r("xk", lo, hi), key(lo, hi), OP.min)
+            act(r("hit", lo, hi), r("m", lo, hi), AF.Sign, bias=r("thb" if t else "th4"), scale=-1.0)
+        mm(c2, r("ID"), r("ci"), True, False)
         for p in range(16):
-            mm(c2, Z("Z4", p), r("hit", p, 256, 16), False, p == 15)
+            mm(c2, Z("ZC", p), r("hit", p, 256, 16), False, p == 15)
         ts(r("F"), r("m"), TW - 1, OP.bitwise_and)
         ts(r("fit"), c2, 128.0, OP.is_lt)
         ts(r("nf"), c2, 128.0, OP.is_ge, float(TW + 1), OP.mult)
@@ -461,13 +480,8 @@ def rank_program(g, core, T, topo):
         tt(r("top"), r("cum"), c2, OP.max)
         ts(r("pos"), r("top"), off, OP.add, r("rF"), OP.add)
         w0 = 64 * (3 - t)
-        scatter(r("SND", w0, w0 + 4352), r("pos"), r("m"))
-        dst, src = T.cores[(rank + 1 + t % (N - 1)) % N], T.cores[(rank - 1 - t % (N - 1)) % N]
-        rid, pid = topo.addr(dst, core)
-        op("G", lambda t=t, w0=w0, dst=dst, rid=rid, pid=pid: g.remote_dma(
-            ap(r("ARR", 64 * t, 64 * t + 64)), ap(r("SND", w0, w0 + 64)), T.sem["arr%d" % t], T.sem["snd"], pid, rid, topo.mask(core, dst)),
-           [r("SND", w0, w0 + 64)], [r("ARR", 64 * t, 64 * t + 64)], 0.05, late=FLIGHT,
-           send=(len(topo.engines(core, dst)), ("arr%d" % t, len(topo.engines(src, core)))))
+        scatter(r("SND", w0, w0 + 4352), r("pos"), r("F"))
+        send(r("ARR", 64 * t, 64 * t + 64), r("SND", w0, w0 + 64), "arr%d" % t, 1 + t % (N - 1), FLIGHT)
         tt(v1, v1, r("fit"), OP.add)
         tt(r("vs"), v1, r("nf"), OP.add)
         ts(r("VS"), r("vs"), -2.0, OP.add)
@@ -478,30 +492,34 @@ def rank_program(g, core, T, topo):
             mm(tot, r("ON"), col("cum", 15), True, True)
             ts(col("bI", 0), tot, 128.0, OP.add)
             ts(col("bI", 1), col("bI", 0), 255, OP.bitwise_and)
-            ts(r("thb"), col("bI", 1), 4096.0, OP.mult, r("th4"), OP.add)
+            act(r("thb"), col("bI", 1), AF.Identity, bias=r("th4"), scale=4096.0)
             tt(vt, vt, r("fit"), OP.add)
             ts(v0L, v1, -1.0, OP.add)
             cp(v1L, v1)
             cp(vtL, vt)
             cp(aL, aw)
             act(r("q"), (r("X2", 0, TW), v0L))
-            ready(r("q"), NG)
-        scatter(r("AA"), r("VS"), r("aB"))
+            ready("q", t + 1)
+            scatter(r("AA"), r("VS"), r("aB"))
+        if t == 2:
+            for s in range(4):
+                act(r("YA", s, 1024, 4), r("AA", s, TW, 8))
+            ts(r("y4"), r("XI", 64, 80), -0.5, OP.mult, -1.0, OP.add)
+            tt(r("y0"), v1, r("y4"), OP.add)
+    tt(r("y4"), r("y0"), r("nf"), OP.add)
+    cp(r("YL"), r("y4"))
+    scatter(r("YA"), r("YL"), r("aB"))
 
-    dma("Y", T["ya"][:], T["W"][:, 0:16], [aw], [], "oL", 8 * KB)
     ts(r("YV"), v1, -1.0, OP.add)
-    dma("Y", T["yv"][:], T["YV"][:], [r("YV")], [], "oV", 8 * KB)
     for s in range(2):
         act(r("pD%d" % s, 0, 256), r("R", 2 + s, TW, 8), AF.Copy, scale=4096.0)
         tt(r("YR", s, 512, 2), r("pD%d" % s, 0, 256), r("R", s, TW, 8), OP.add)
-    dma("Y", T["yr"][:], T["YR"][:], [r("YR")], [], "oR", 256 * KB)
-    for s in range(4):
-        act(r("YA", s, 1024, 4), r("AA", s, TW, 8))
-    dma("S", T["yan"][:], T["YA"][0::16, :], [r("YA")], [], "oA", 32 * KB)
-    for t in range(3):
-        act(r("YH", t, 256, 4), r("R", 4 + t, TW, 32))
-    tt(r("bt"), r("ARR", 192, 256), r("R", 7, TW, 32), OP.min)
-    ts(r("b3"), r("bt"), TW - 1, OP.bitwise_and)
-    cp(r("YH", 3, 256, 4), r("b3"))
-    dma("Y", T["yh"][:], T["YH"][:], [r("YH")], [], "oH", 128 * KB)
+    for t in range(4):
+        act(r("YH", t, 256, 4), r("ARR", 64 * t, 64 * t + 64))
+    outs = {"L": ("Y", T["ya"][:], T["W"][:, 0:16], aw, 8), "V": ("Y", T["yv"][:], T["YV"][:], r("YV"), 8),
+            "R": ("Y", T["yr"][:], T["YR"][:], r("YR"), 256), "A": ("Y", T["yan"][:], T["YA"][0::16, 0:1024], r("YA"), 32),
+            "H": ("S", T["yh"][:], T["YH"][:], r("YH"), 128)}
+    for x in OUTS:
+        eng, o, a, reg, size = outs[x]
+        dma(eng, o, a, [reg], [], "o" + x, size * KB)
     issue()

from concourse.mybir import AluOpType as OP, ActivationFunctionType as AF

TW = 2048
BIG = float(1 << 25)
K0 = -255 << 15
KV = 9
NQ = 64
PIECES = (64, 96, 128, 160, 192, 224, 32, 0)
WHO = ("VSVSVVVV", "VSVSVVqq", "VSVSVVqq", "VSVSVVqq")
SUMS = ((64, 128), (128, 192), (192, 256), (0, 64))
TAIL = ((64, 256), (0, 64))
XB = "DD"
NBS, PAIR, ES, NM = 2, 2, "VVVV", 4
OUTS = "VLRHA"
CYC, GATHER, SCATTER, PEC, HOP, DFIX, DBW, FLIGHT, ROUNDS = 0.00083, 1.4, 3.0, 0.00042, 0.11, 0.9, 350e3, 2.0, 4
SCRATCH = {}
for _n, _w, _d in (
    ("X2", 4096, "bfloat16"), ("R", 4096, "int32"), ("AA", 4096, "int32"), ("IOT", 2048, "int32"), ("SXS", 2048, "float32"),
    ("KN", 1024, "float32"), ("QS", 2048, "bfloat16"), ("MX", 8192, "bfloat16"), ("XS", 4096, "bfloat16"),
    ("QX", 16 * NQ, "bfloat16"), ("XG", 4096, "bfloat16"), ("DD", 16 * NQ, "bfloat16"), ("AD", 4096, "bfloat16"),
    ("SND", 4608, "int32"), ("ARR", 256, "int32"), ("OLD", 256, "int32"), ("sx", 256, "float16"),
    ("q", 256, "bfloat16"), ("QT", 256, "bfloat16"), ("AB", 512, "float16"), ("aB", 256, "float32"), ("e", 256, "float16"),
    ("prod", 256, "int32"), ("pl", 256, "int32"), ("pl16", 256, "uint16"), ("pen", 256, "float32"), ("xk", 256, "float32"),
    ("m", 256, "int32"), ("hit", 256, "bfloat16"), ("F", 256, "int32"),
    ("fit", 16, "float32"), ("cum", 16, "bfloat16"), ("top", 16, "float32"), ("pos", 16, "uint16"), ("nf", 16, "float32"),
    ("vs", 16, "float32"), ("VS", 16, "uint16"), ("Aw", 32, "float32"), ("dA", 16, "float32"), ("tA", 16, "float32"),
    ("W", 48, "float32"), ("AL", 64, "uint16"), ("bI", 2, "int32"), ("th4", 1, "float32"), ("thb", 1, "float32"),
    ("thI", 1, "int32"), ("wI", 1, "int32"), ("wF", 1, "float32"),
    ("pI", 1, "int32"), ("pF", 1, "float32"), ("rI", 1, "int32"), ("rF", 1, "float32"), ("q16", 1, "float32"),
    ("nr0", 1, "float32"), ("lu", 1, "float32"), ("nb", 1, "float32"), ("kI", 2, "int32"), ("ck", 1, "float32"),
    ("OH", 16, "float32"), ("CI", 144, "float32"), ("CB", 128, "float32"), ("C16", 16, "float32"), ("XI", 128, "int32"),
    ("XL", 64, "uint16"), ("ci", 16, "bfloat16"), ("r32", 1, "int32"), ("p32", 1, "float32"), ("EI", 512, "bfloat16"),
    ("E", 512, "bfloat16"), ("Z1", 144, "bfloat16"), ("Z4", 144, "bfloat16"), ("ZW", 144, "bfloat16"), ("ZA", 144, "bfloat16"),
    ("ZC", 144, "bfloat16"), ("BO", 128, "bfloat16"), ("BO2", 128, "bfloat16"), ("BN", 128, "bfloat16"), ("BP", 128, "bfloat16"),
    ("LU", 128, "bfloat16"), ("LO", 128, "bfloat16"), ("PD", 128, "bfloat16"), ("PB", 128, "bfloat16"), ("LT", 128, "bfloat16"),
    ("ID", 128, "bfloat16"), ("NI", 128, "bfloat16"), ("IZ", 128, "bfloat16"), ("N2", 128, "bfloat16"),
    ("ON", 128, "bfloat16"), ("ZR", 128, "bfloat16"),
    ("AC", 128, "int32"), ("OC", 128, "int32"), ("uI", 128, "int32"), ("uA", 128, "int32"), ("uM", 128, "int32"),
    ("u32", 128, "float32"), ("SXT", 128, "float32"),
    ("YR", 512, "float32"), ("YH", 256, "float32"), ("YA", 3088, "float32"), ("YV", 16, "float32"),
    ("y0", 16, "float32"), ("y4", 16, "float32"), ("YL", 16, "uint16"),
):
    SCRATCH[_n] = ("sbuf", [128, _w], _d)
SCRATCH["OL"] = ("sbuf", [128, 4, 256], "uint16")
SCRATCH["pr"] = SCRATCH["bs"] = ("sbuf", [128, 4, 16], "int32")
SCRATCH["SXD"] = ("dram", [8, 2 * TW], "float32")
PSUM = ("pK", "pE", "pO", "pD0", "pD1", "pD2", "pC", "pW")
for _n in PSUM:
    SCRATCH[_n] = ("psum", [128, 512], "float32")
DMAS = {"lAC": 1, "lOC": 1, "lW": 1, "lT": 1, "lX0": 1, "lX1": 1, "lB0": 1, "lB1": 1, "lR": 1, "gAA": 3, "gSD": 2, "gSX": 16,
        "oR": 1, "oH": 1, "oA": 1, "oV": 1, "oL": 1}
SEMAPHORES = ["V", "S", "P", "G", "snd"] + [x + str(t) for x in ("arr", "pre") for t in range(4)] + list(DMAS)
_ORDER = []


def _meet(a, b):
    if a[0] >= b[1] or b[0] >= a[1]:
        return False
    if a[2] == b[2]:
        return a[2] == 1 or (a[0] - b[0]) % a[2] == 0
    if a[2] == 1 or b[2] == 1:
        if b[2] == 1:
            a, b = b, a
        first = b[0] + max(0, -((b[0] - a[0]) // b[2])) * b[2]
        return first < min(a[1], b[1])
    return True


def _covers(a, b):
    return a == b or (a[2] == 1 and a[0] <= b[0] and a[1] >= b[1])


def _place(busy, t, d):
    for n, (a, b) in enumerate(busy):
        if t + d <= a:
            busy.insert(n, (t, t + d))
            return t
        t = max(t, b)
    busy.append((t, t + d))
    return t


def _order(calls):
    every, best = range(len(calls)), None
    way = [0.0 for _ in every]
    for i in reversed(every):
        c = calls[i]
        way[i] += c["cost"] + c["late"]
        for j in c["wait"]:
            way[j] = max(way[j], way[i] + HOP)
        for j in c["after"]:
            way[j] = max(way[j], way[i] - calls[j]["late"])
    for _ in range(ROUNDS):
        busy = {k: [] for k in "VSPGY"}
        start, free, done, rings = {}, {}, {}, 0.0
        for i in sorted(every, key=lambda i: (-way[i], i)):
            c = calls[i]
            t = max([0.0] + [done[j] + HOP for j in c["wait"]] + [free[j] for j in c["after"]])
            start[i] = _place(busy[c["eng"]], t, c["cost"])
            free[i] = start[i] + c["cost"]
            done[i] = free[i] + c["late"]
            if c["ring"]:
                rings = max(rings, free[i] + DFIX / 2) + c["ring"]
                done[i] = rings + DFIX / 2
        if best is None or max(done.values()) < best[0]:
            best = (max(done.values()), sorted(every, key=lambda i: (start[i], i)))
        busy = {k: [] for k in "VSPGY"}
        back = [calls[i]["late"] for i in every]
        for i in sorted(every, key=lambda i: (-free[i], -i)):
            c = calls[i]
            way[i] = _place(busy[c["eng"]], back[i], c["cost"]) + c["cost"]
            for j in c["wait"]:
                back[j] = max(back[j], way[i] + HOP + done[j] - free[j])
            for j in c["after"]:
                back[j] = max(back[j], way[i])
    return best[1]


def rank_program(g, core, T, topo):
    rank = T.rank_of(core)
    if rank is None:
        return
    N = len(T.cores)
    Q = {"V": g.vector, "S": g.scalar, "P": g.tensor, "G": g, "Y": g.sync}
    calls, log, groups, lastdma = [], {}, {}, {}

    def r(name, lo=0, hi=None, st=1):
        return (name, lo, SCRATCH[name][1][1] if hi is None else hi, st)

    def rp(name, lo, hi, p0, p1):
        return (name, lo, hi, 1, p0, p1)

    def ap(x):
        if len(x) == 2:
            return ap(x[0]).indirect(ap(x[1]))
        if len(x) == 6:
            return T[x[0]][x[4]:x[5], x[1]:x[2]]
        n, lo, hi, st = x
        if len(SCRATCH[n][1]) == 3:
            w = SCRATCH[n][1][2]
            return T[n][:, lo // w, lo % w:lo % w + hi - lo]
        return T[n][:, lo:hi:st] if st > 1 else T[n][:, lo:hi]

    def flat(xs):
        out = []
        for x in xs:
            if isinstance(x, tuple):
                if len(x) == 2:
                    out += [x[0], x[1]]
                else:
                    out.append(x[:4])
        return out

    def width(x):
        return 16 * width(x[1]) if len(x) == 2 else -((x[1] - x[2]) // x[3])

    def short(*xs):
        return all(SCRATCH[x[0]][2].endswith("16") for x in xs)

    def op(eng, fn, reads, writes, cost, grp=None, late=0.0, ring=0.0, send=None):
        me = len(calls)
        uses = [(x, False) for x in flat(reads)] + [(x, True) for x in flat(writes)]
        wait, after = {}, set()
        for acc, wr in uses:
            bank = acc[0] in PSUM
            for (sp, w2, j) in log.get(acc[0], ()):
                c = calls[j]
                if grp is not None and c["grp"] == grp:
                    continue
                if bank and c["eng"] == eng == "P":
                    after.add(j)
                elif (bank and c["eng"] != eng) or ((wr or w2) and _meet(acc[1:], sp)):
                    for k in groups.get(c["grp"], [j]):
                        wait[k] = acc[0]
        if ring or send:
            if bool(ring) in lastdma:
                after.add(lastdma[bool(ring)])
            lastdma[bool(ring)] = me
        if grp is not None:
            groups.setdefault(grp, []).append(me)
        calls.append(dict(eng=eng, fn=fn, cost=cost, late=late + (ring and ring + DFIX), ring=ring, grp=grp, send=send, wait=wait, after=after))
        for acc, wr in uses:
            keep = [rec for rec in log.get(acc[0], ())
                    if not (wr and _covers(acc[1:], rec[0]) and (grp is None or calls[rec[2]]["grp"] != grp))]
            if acc[0] in PSUM and eng == "P":
                keep = [rec for rec in keep if rec[2] not in wait and rec[2] not in after]
            log[acc[0]] = keep + [(acc[1:], wr, me)]

    def issue():
        if not _ORDER:
            _ORDER.extend(_order(calls))
        count = {k: 0 for k in "VSPG"}
        known = {k: {} for k in Q}
        mark = {}
        sent = 0
        for i in _ORDER:
            c = calls[i]
            kn = known[c["eng"]]
            need = [mark[j].get(name, mark[j][""]) for j, name in c["wait"].items()]
            for sem, val, clock in sorted(need, key=lambda x: (-len(x[2]), -x[1])):
                if kn.get(sem, 0) < val:
                    Q[c["eng"]].wait_ge(T.sem[sem], val)
                    for s, x in list(clock.items()) + [(sem, val)]:
                        kn[s] = max(kn.get(s, 0), x)
            ins = c["fn"]()
            if c["send"]:
                out, tile, sem, inn = c["send"]
                sent += out
                mark[i] = {"": ("snd", sent, dict(kn)), tile: (sem, inn, {})}
            elif c["grp"] is not None:
                ins.then_inc(T.sem[c["grp"]], 16)
                mark[i] = {"": (c["grp"], 16 * DMAS[c["grp"]], dict(kn))}
            else:
                count[c["eng"]] += 1
                ins.then_inc(T.sem[c["eng"]], 1)
                mark[i] = {"": (c["eng"], count[c["eng"]], dict(kn))}
        for grp in groups:
            g.wait_ge(T.sem[grp], 16 * DMAS[grp])
        for e in "VSPG":
            g.wait_ge(T.sem[e], count[e])
        g.wait_ge(T.sem["snd"], sent)

    def sc(x):
        return ap(x) if isinstance(x, tuple) else x

    def vcost(a, per):
        if len(a) == 2:
            return 0.05 + CYC * GATHER * width(a)
        return 0.02 + CYC * max(64, per * width(a))

    def tt(o, a, b, f):
        per = 1 if a[0] in PSUM or b[0] in PSUM else 2
        op("V", lambda: g.vector.tensor_tensor(out=ap(o), in0=ap(a), in1=ap(b), op=f), [a, b], [o], vcost(a, per))

    def ts(o, a, s1, f, s2=None, f2=None):
        kw = {} if f2 is None else {"op1": f2}
        op("V", lambda: g.vector.tensor_scalar(out=ap(o), in0=ap(a), scalar1=sc(s1), scalar2=sc(s2), op0=f, **kw), [a, s1, s2], [o],
           vcost(a, 0.5 if short(o, a) else 1))

    def cp(o, a):
        op("V", lambda: g.vector.tensor_copy(out=ap(o), in_=ap(a)), [a], [o], vcost(a, 0.5 if len(a) > 2 and short(o, a) else 1))

    def scatter(win, off, a):
        op("V", lambda: g.vector.tensor_copy(out=ap((win, off)), in_=ap(a)), [a, off], [win], 0.05 + CYC * SCATTER * width(a))

    def act(o, a, f=AF.Copy, bias=None, scale=None):
        kw = {}
        if bias is not None:
            kw["bias"] = sc(bias)
        if scale is not None:
            kw["scale"] = sc(scale)
        op("S", lambda: g.scalar.activation(out=ap(o), in_=ap(a), func=f, **kw), [a, bias, scale], [o],
           0.06 + CYC * max(64, width(a) * (GATHER if len(a) == 2 else 1)))

    def move(eng, o, a):
        (cp if eng == "V" else act)(o, a)

    def mm(o, l, x, start, stop):
        op("P", lambda: g.tensor.matmul(out=ap(o), lhsT=ap(l), rhs=ap(x), start=start, stop=stop), [l, x], [o],
           0.01 + PEC * max(64, width(x)))

    def dma(eng, out, in_, reads, writes, grp, size):
        op(eng, lambda: Q[eng].dma_start(out=out, in_=in_), reads, writes, 0.05, grp, ring=0.13 + size / DBW)

    def send(o, a, sem, step, late):
        dst, src = T.cores[(rank + step) % N], T.cores[(rank - step) % N]
        rid, pid = topo.addr(dst, core)
        op("G", lambda: g.remote_dma(ap(o), ap(a), T.sem[sem], T.sem["snd"], pid, rid, topo.mask(core, dst)), [a], [o], 0.05,
           late=late, send=(len(topo.engines(core, dst)), o[0], sem, len(topo.engines(src, core))))

    def iota(o, pattern, cm, base=0):
        op("G", lambda: g.iota(ap(o), pattern, base, cm, allow_small_or_imprecise_dtypes=True), [], [o], 0.13 + 2 * CYC * width(o))

    def sel(o, a, pattern, cmp, base, cm, other=0.0):
        op("G", lambda: g.affine_select(ap(o), ap(a), pattern, cmp, other, base, cm), [a], [o], 0.17 + 2 * CYC * width(o))

    def gcp(o, a):
        sel(o, a, [[0, width(o)]], OP.is_equal, 0, 0)

    def Z(name, k):
        return r(name, 15 - k, 143 - k)

    def col(name, c):
        return r(name, c, c + 1)

    aL, v1L, vtL, v0L = (r("AL", 16 * n, 16 * n + 16) for n in range(4))
    aw, v1, vt = (r("W", 16 * n, 16 * n + 16) for n in range(3))
    MV = r("AB", 256, 512)
    u, pd = r("pE", 0, 256), r("pE", 256, 512)
    c2, off, tot = r("pC", 0, 16), col("pE", 256), col("pE", 257)
    KB = 1024

    dma("S", T["wI"][:], T["w"][:], [], [r("wI")], "lW", 512)
    for h in range(2):
        dma("YS"[h], T["X2"][:, KB * h:KB * h + KB], T["xc"][:, KB * h:KB * h + KB], [], [r("X2", KB * h, KB * h + KB)], "lX%d" % h, 256 * KB)
    dma("Y", T["OC"][:], T["rf"][0::16, :], [], [r("OC")], "lOC", 64 * KB)
    dma("S", T["AC"][:], T["an"][:], [], [r("AC")], "lAC", 64 * KB)
    for h in range(2):
        one, two = r("X2", KB * h, KB * h + KB), r("X2", TW + KB * h, TW + KB * h + KB)
        if XB[h] == "D":
            dma("Y", ap(two), T["xc"][:, KB * h:KB * h + KB], [], [two], "lB%d" % h, 256 * KB)
        else:
            move(XB[h], two, one)
    dma("Y", T["R"][:, 0:TW], T["rf"][:], [], [r("R", 0, TW)], "lR", KB * KB)
    dma("Y", T["thI"][:], T["th"][:], [], [r("thI")], "lT", 512)

    for h in range(4):
        x = r("AA", 512 * h, 512 * h + 512)
        if h < NM:
            op("V", lambda x=x: g.vector.memset(ap(x), 1), [], [x], CYC * 512)
        else:
            iota(x, [[0, 512]], 0, 1)
    iota(r("pI"), [[1, 1]], 1)
    iota(r("pF"), [[1, 1]], 1)
    iota(r("CI"), [[1, 144]], 0)
    iota(r("XI", 0, 64), [[1, 4], [8, 16]], 128)
    iota(r("CB"), [[16, 8], [0, 16]], 0)
    iota(r("C16"), [[16, 16]], 0)
    iota(r("EI"), [[1, 32], [0, 16]], 0)
    iota(r("ZR"), [[0, 128]], 0)
    iota(r("ON"), [[0, 128]], 0, 1)
    for h in range(4):
        iota(r("IOT", 512 * h, 512 * h + 512), [[1, 512]], 0, 512 * h)
    ts(r("rI"), r("pI"), 15, OP.bitwise_and)
    ts(r("XI", 64, 128), r("XI", 0, 64), TW - 1, OP.bitwise_and)
    cp(r("rF"), r("rI"))
    cp(r("XL"), r("XI", 64, 128))
    tt(r("q16"), r("pF"), r("rF"), OP.subtract)
    act(r("wF"), r("wI"))
    ts(r("r32"), r("pI"), 31, OP.bitwise_and)
    ts(r("Z1"), r("CI"), -15.0, OP.add, r("q16"), OP.is_equal)
    ts(r("OH"), r("CI", 0, 16), r("rF"), OP.is_equal)
    ts(r("ID"), r("CI", 0, 128), r("pF"), OP.is_equal)
    ts(r("BO"), r("CB"), r("q16"), OP.is_equal)
    cp(r("p32"), r("r32"))
    ts(v1, r("XI", 64, 80), 1.0, OP.add)
    ts(vt, r("C16"), r("rF"), OP.add, 4.0, OP.mult)
    ts(r("lu"), col("OH", 4), 2080.0, OP.mult, col("OH", 3), OP.add)
    ts(r("nr0"), r("rF"), 0.0, OP.not_equal)
    ts(r("nb"), col("OH", 0), -BIG, OP.mult)
    cp(r("AL", 16, 48), r("W", 16, 48))
    cp(aL, r("AC", 0, 128, 8))
    ts(col("kI", 0), r("rI"), 613.0, OP.mult)
    ts(col("kI", 1), col("kI", 0), TW - 1, OP.bitwise_and)
    cp(r("ck"), col("kI", 1))
    ts(r("E"), r("EI"), r("p32"), OP.is_equal, -1.0, OP.mult)
    ts(r("ci"), r("XI", 64, 80), 0.125, OP.mult, -256.0, OP.add)
    ts(r("th4"), r("thI"), 4096.0, OP.mult, K0 - 0.5, OP.add)
    for o, a, x in (("ZW", "Z1", r("wF")), ("Z4", "Z1", 4096.0), ("ZC", "Z1", -256.0), ("ZA", "Z1", col("OH", 0)),
                    ("NI", "ID", -1.0), ("N2", "ID", -2048.0), ("IZ", "ID", r("nr0")), ("PD", "ID", BIG),
                    ("LU", "BO", r("lu")), ("BO2", "BO", col("OH", 2)), ("PB", "BO", r("nb")), ("BN", "BO", -2048.0), ("BP", "BO", 4096.0)):
        act(r(o), r(a), AF.Copy, scale=x)
    tt(r("PD"), r("PD"), r("PB"), OP.add)
    sel(r("BP"), r("BP"), [[0, 8], [1, 16]], OP.is_ge, -KV, 0)
    sel(r("LO"), r("ZR"), [[-16, 8], [-1000, 16]], OP.not_equal, -2, 1, 1.0)
    sel(r("LO"), r("LO"), [[-16, 8], [0, 16]], OP.not_equal, -4, 1, float(K0))
    sel(r("LT"), r("BO"), [[1, 128]], OP.is_gt, 0, -1)
    act(r("KN"), r("X2", 0, KB), AF.Copy, scale=0.0)
    dma("Y", T["AA"][0::16, 0:TW], T["an"][:], [], [r("AA", 0, TW)], "gAA", 64 * KB)
    dma("Y", T["AA"][2::16, 1:TW + 1], T["rf"][0::16, :], [], [r("AA", 1, TW + 1)], "gAA", 64 * KB)
    for t in range(4):
        old = r("OLD", 64 * t, 64 * t + 64)
        gcp(old, r("R", 4 + t, TW, 32))
        send(r("SND", 192 - 64 * t, 256 - 64 * t), old, "pre%d" % t, -1 - t % (N - 1), 3 * FLIGHT + 13 * t)

    def ol(s, k, n=1):
        return r("OL", 256 * s + 16 * k, 256 * s + 16 * (k + n))

    def own(s):
        o, m0 = r("pO", 0, 256), 4096 * (s % 2)
        mm(o, r("BN"), r("QS", 512 * s, 512 * s + 256), True, False)
        mm(o, r("BP"), r("QS", 512 * s, 512 * s + 256), False, False)
        act(r("sx"), (r("SXS"), ol(s, 0)))
        ks = [(k, min(PAIR, KV - k)) for k in range(0, KV, PAIR)]
        for n, k in enumerate(range(KV, 16, 2)):
            ks.insert((4 - PAIR) * n + 1, (k, min(2, 16 - k)))
        for k, n in ks:
            mx, qs = r("MX", m0 + 256 * k, m0 + 256 * (k + n)), r("QS", 512 * s, 512 * s + 256 * n)
            if k < KV:
                tt(mx, (r("X2"), ol(s, k, n)), qs, OP.max)
            else:
                xs, b = r("XS", 256 * k, 256 * (k + n)), r("pD%d" % (2 - (k - KV) // 2 % NBS), 0, 256 * n)
                act(xs, (r("X2"), ol(s, k, n)))
                mm(b, r("ID"), xs, True, False)
                mm(b, r("NI"), qs, False, True)
                act(mx, b, AF.Relu)
            for h in range(n):
                mm(o, Z("Z4", k + h), r("MX", m0 + 256 * (k + h), m0 + 256 * (k + h + 1)), False, False)
        mm(o, r("N2"), r("sx"), False, True)
        act(r("KN", s, 1024, 4), o, AF.Identity, bias=float(2048 - (1 << 23) + K0), scale=2.0)

    def key(lo, hi):
        return r("pK", lo, hi) if TAIL[0][0] <= lo < TAIL[0][1] else r("pC", 256 + lo, 256 + hi)

    def ready(q, t):
        for h in range(2):
            mm(r("pW", 128 + 128 * h, 256 + 128 * h), r(q, 128 * h, 128 * h + 128), r("ID"), True, True)
        act(r("QT"), r("pW", 128, 384))
        for k in range(16 if "q" in WHO[t] else 0):
            gcp(r("QX", k, 16 * NQ, 16), r(q, 0, NQ))
        act(MV, (r("AA", 0, TW), v1L))
        mm(u, r("LU"), MV, True, True)

    for p in range(16):
        mm(r("pW", 0, 128), Z("ZW", p), r("X2", 128 * p, 128 * p + 128), p == 0, p == 15)
    for p in range(16):
        mm(r("pC", 0, 128), Z("Z1", p), r("X2", 128 * p, 128 * p + 128), p == 0, p == 15)
    for s in range(4):
        one, two = r("QS", 512 * s, 512 * s + 256), r("QS", 512 * s + 256, 512 * s + 512)
        act(one, (r("X2", 0, TW), r("XL", 16 * s, 16 * s + 16)))
        (gcp if s else cp)(two, one)
    cp(r("uI"), r("pW", 0, 128))
    ts(r("uA"), r("uI"), 4095, OP.bitwise_and)
    ts(r("u32"), r("uA"), 32.0, OP.add)
    ts(r("uM"), r("uA"), -2048.0, OP.add)
    act(r("SXT"), r("pC", 0, 128), AF.Identity, bias=-2048.0)
    for s in range(4):
        tt(r("pr", 16 * s, 16 * s + 16), r("u32", s, 128, 8), r("OC", s, 128, 8), OP.mult)
    dma("Y", T["AA"][3::16, 1:TW + 1], T["uM"][:], [r("uM")], [r("AA", 1, TW + 1)], "gAA", 64 * KB)
    for h in range(2):
        dma("Y", T["SXD"][:, TW * h:TW * h + TW], T["SXT"][:], [r("SXT")], [r("SXD", TW * h, TW * h + TW)], "gSD", 64 * KB)
    for k in range(16):
        d = 613 * k % TW
        dma("Y", T["SXS"][k::16, :], T["SXD"][:, d:d + TW], [r("SXD")], [r("SXS")], "gSX", 64 * KB)
    op("V", lambda: g.vector.tensor_scalar(out=T["bs"][:], in0=T["pr"][:], scalar1=5, scalar2=TW - 1, op0=OP.arith_shift_right,
                                           op1=OP.bitwise_and), [r("pr", 0, 64)], [r("bs", 0, 64)], 0.07)
    for k in range(16):
        op("V", lambda k=k: g.vector.tensor_scalar(out=T["OL"][:, :, 16 * k:16 * k + 16], in0=T["bs"][:], scalar1=float(613 * k % TW),
                                                   scalar2=None, op0=OP.add), [r("bs", 0, 64)], [ol(s, k) for s in range(4)], 0.07)
    ready("QS", 0)

    for t in range(4):
        own(t)
        if t > 0:
            cp(r("R", 4 + t - 1, TW, 32), r("ARR", 64 * t - 64, 64 * t))
        move(ES[t], r("e"), (r("R", 0, TW), aL))
        tt(r("prod"), r("e"), u, OP.mult)
        ts(r("pl"), r("prod"), 5, OP.arith_shift_right, TW - 1, OP.bitwise_and)
        ts(r("pl16"), r("pl"), r("ck"), OP.add)
        for lo, hi in TAIL:
            mm(key(lo, hi), r("IZ"), r("e", lo, hi), True, False)
            mm(key(lo, hi), r("LO"), r("AB", 256 + lo, 256 + hi), False, False)
        mm(pd, r("PD"), r("e"), True, False)
        mm(pd, r("BO2"), MV, False, True)
        act(r("pen"), pd, AF.Abs)
        tt(r("xk"), (r("KN"), vtL), r("pen"), OP.add)
        for a, who in zip(PIECES, WHO[t]):
            x, lo, hi = (r("X2"), r("pl16", a, a + 32)), 16 * a, 16 * a + 512
            if who == "q":
                tt(r("DD", lo, hi), x, r("QX", lo, hi), OP.subtract)
                act(r("AD", lo, hi), r("DD", lo, hi), AF.Abs)
            else:
                b, h, p = r("pD%d" % (a // 32 % 3)), a // 128, a % 128
                move(who, r("XG", lo, hi), x)
                mm(b, r("ID"), r("XG", lo, hi), True, False)
                mm(b, rp("QT", 128 * h, 128 * h + 128, p, p + 32), rp("E", 0, 512, p, p + 32), False, True)
                act(r("AD", lo, hi), b, AF.Abs)
        for n, (lo, hi) in enumerate(SUMS):
            last = all(key(*x)[0] != key(lo, hi)[0] for x in SUMS[n + 1:])
            for k in range(16):
                mm(key(lo, hi), Z("Z4", k), r("AD", 16 * lo + k, 16 * hi, 16), False, last and k == 15)
        act(r("AB", 0, 256), (r("AA", 0, TW), aL))
        for p in range(16):
            mm(r("pW", 0, 32), Z("ZA", p), r("AB", p, 512, 16), p == 0, p == 15)
        act(r("Aw"), r("pW", 0, 32))
        act(r("aB"), (r("IOT"), aL))
        tt(r("dA"), r("Aw", 16, 32), r("Aw", 0, 16), OP.subtract)
        for lo, hi in TAIL:
            tt(r("m", lo, hi), r("xk", lo, hi), key(lo, hi), OP.min)
            act(r("hit", lo, hi), r("m", lo, hi), AF.Sign, bias=r("thb" if t else "th4"), scale=-1.0)
        mm(c2, r("ID"), r("ci"), True, False)
        for p in range(16):
            mm(c2, Z("ZC", p), r("hit", p, 256, 16), False, p == 15)
        ts(r("F"), r("m"), TW - 1, OP.bitwise_and)
        ts(r("fit"), c2, 128.0, OP.is_lt)
        ts(r("nf"), c2, 128.0, OP.is_ge, float(TW + 1), OP.mult)
        op("V", lambda: g.vector.tensor_tensor_scan(ap(r("cum")), ap(r("fit")), ap(r("ZR", 0, 16)), -1.0, OP.add, OP.add),
           [r("fit"), r("ZR", 0, 16)], [r("cum")], 0.07)
        mm(off, r("LT"), col("cum", 15), True, True)
        tt(r("top"), r("cum"), c2, OP.max)
        ts(r("pos"), r("top"), off, OP.add, r("rF"), OP.add)
        w0 = 64 * (3 - t)
        scatter(r("SND", w0, w0 + 4352), r("pos"), r("F"))
        send(r("ARR", 64 * t, 64 * t + 64), r("SND", w0, w0 + 64), "arr%d" % t, 1 + t % (N - 1), FLIGHT)
        tt(v1, v1, r("fit"), OP.add)
        tt(r("vs"), v1, r("nf"), OP.add)
        ts(r("VS"), r("vs"), -2.0, OP.add)
        tt(r("tA"), r("fit"), r("dA"), OP.mult)
        tt(aw, r("tA"), r("Aw", 0, 16), OP.add)
        scatter(r("R"), r("VS"), r("F"))
        if t < 3:
            mm(tot, r("ON"), col("cum", 15), True, True)
            ts(col("bI", 0), tot, 128.0, OP.add)
            ts(col("bI", 1), col("bI", 0), 255, OP.bitwise_and)
            act(r("thb"), col("bI", 1), AF.Identity, bias=r("th4"), scale=4096.0)
            tt(vt, vt, r("fit"), OP.add)
            ts(v0L, v1, -1.0, OP.add)
            cp(v1L, v1)
            cp(vtL, vt)
            cp(aL, aw)
            act(r("q"), (r("X2", 0, TW), v0L))
            ready("q", t + 1)
            scatter(r("AA"), r("VS"), r("aB"))
        if t == 2:
            for s in range(4):
                act(r("YA", s, 1024, 4), r("AA", s, TW, 8))
            ts(r("y4"), r("XI", 64, 80), -0.5, OP.mult, -1.0, OP.add)
            tt(r("y0"), v1, r("y4"), OP.add)
    tt(r("y4"), r("y0"), r("nf"), OP.add)
    cp(r("YL"), r("y4"))
    scatter(r("YA"), r("YL"), r("aB"))

    ts(r("YV"), v1, -1.0, OP.add)
    for s in range(2):
        act(r("pD%d" % s, 0, 256), r("R", 2 + s, TW, 8), AF.Copy, scale=4096.0)
        tt(r("YR", s, 512, 2), r("pD%d" % s, 0, 256), r("R", s, TW, 8), OP.add)
    for t in range(4):
        act(r("YH", t, 256, 4), r("ARR", 64 * t, 64 * t + 64))
    outs = {"L": ("Y", T["ya"][:], T["W"][:, 0:16], aw, 8), "V": ("Y", T["yv"][:], T["YV"][:], r("YV"), 8),
            "R": ("Y", T["yr"][:], T["YR"][:], r("YR"), 256), "A": ("Y", T["yan"][:], T["YA"][0::16, 0:1024], r("YA"), 32),
            "H": ("S", T["yh"][:], T["YH"][:], r("YH"), 128)}
    for x in OUTS:
        eng, o, a, reg, size = outs[x]
        dma(eng, o, a, [reg], [], "o" + x, size * KB)
    issue()
